import numpy as np
import ml_dtypes


def mxq(x, axis, fmt="e4m3"):
    dtype, down = {"e4m3": (ml_dtypes.float8_e4m3fn, 7), "e5m2": (ml_dtypes.float8_e5m2, 14)}[fmt]
    v = np.moveaxis(np.asarray(x, np.float32).astype(ml_dtypes.bfloat16).astype(np.float64), axis, -1)
    blocks = v.reshape(v.shape[:-1] + (-1, 32))
    amax = np.abs(blocks).max(-1, keepdims=True)
    byte = np.maximum(np.where(amax > 0, np.frexp(amax)[1] - 1 + 127, 0) - down, 1)
    scale = np.exp2(byte - 127.0)
    codes = (blocks / scale).astype(np.float32).astype(dtype).astype(np.float64)
    return np.moveaxis((codes * scale).reshape(v.shape), -1, axis)


WIDE = False


def mx_kscale(k):
    if not WIDE:
        return np.ones(k)
    levels = np.array([10, -10, 5, -5, 0])
    if k % 512:
        return np.exp2(np.random.permutation(np.resize(levels, k // 32))).repeat(32)
    a = np.empty((k // 512, 16))
    for p in range(k // 512):
        a[p, :8] = np.random.permutation(np.resize(levels, 8))
        for g in range(8):
            far = levels[np.abs(levels - a[p, g]) >= 10]
            a[p, g + 8] = far[np.random.randint(len(far))]
    return np.exp2(a.ravel()).repeat(32)


def f64(x):
    return np.asarray(x).astype(np.float64)


def striped(idx):
    return np.tile(idx.reshape(-1, 16).T, (8, 1)).astype(np.uint16)


def unstriped(offs):
    return offs[:16].T.reshape(-1).astype(np.int64)


E2M1 = np.array([0.0, 0.5, 1.0, 1.5, 2.0, 3.0, 4.0, 6.0, -0.0, -0.5, -1.0, -1.5, -2.0, -3.0, -4.0, -6.0])


def pack_fp4(w):
    k, n = w.shape
    w = f64(np.asarray(w, np.float32).astype(ml_dtypes.bfloat16)).reshape(k // 32, 32, n)
    amax = np.abs(w).max(1)
    mant, ex = np.frexp(amax / 6.0)
    byte = np.clip(np.where(amax > 0, np.where(mant > 0.5, ex, ex - 1) + 127, 1), 1, 254)
    scaled = (w * np.exp2(127.0 - byte)[:, None, :]).reshape(k, n).astype(np.float32)
    c = np.ascontiguousarray(scaled.reshape(k // 512, 128, 4, n).transpose(0, 1, 3, 2)).astype(ml_dtypes.float4_e2m1fn).view(np.uint8) & 0xF
    words = (c[..., 0::2] | (c[..., 1::2] << 4)).reshape(k // 512, 128, 2 * n)
    return np.ascontiguousarray(words), np.ascontiguousarray(byte.astype(np.uint8).reshape(k // 512, 16, n))


def unpack_fp4(words, scales):
    g, _, n = scales.shape
    words = np.ascontiguousarray(words).reshape(g, 128, n, 2)
    nib = np.empty((g, 128, n, 4), np.uint8)
    nib[..., 0::2] = words & 0xF
    nib[..., 1::2] = words >> 4
    vals = E2M1[nib] * np.repeat(np.exp2(scales.astype(np.float64) - 127.0), 8, axis=1)[..., None]
    return vals.transpose(0, 1, 3, 2).reshape(g * 512, n)


K, T, S, N, U = 1024, 2048, 1024, 128, 1024


def setup_inputs():
    n = np.random.standard_normal
    s = mx_kscale(K)[:, None]
    packed_w1 = pack_fp4(n((K, N)) / np.sqrt(K) / s)
    packed_w2 = pack_fp4(n((K, N)) / np.sqrt(K) / s)
    packed_w3 = pack_fp4(n((K, N)) / np.sqrt(K) / s)
    return {
        "xT": (n((K, T)) * s).astype(np.float32),
        "w1_words": packed_w1[0],
        "w1_scales": packed_w1[1],
        "w2_words": packed_w2[0],
        "w2_scales": packed_w2[1],
        "w3_words": packed_w3[0],
        "w3_scales": packed_w3[1],
        "offs": striped(np.random.permutation(T)[:S]),
        "src": striped(np.random.permutation(S)[(S * np.random.uniform(0, 1, U) ** 4).astype(np.int64)]),
        "dst": striped(np.random.permutation(S)),
    }


def reference(xT, w1_words, w1_scales, w2_words, w2_scales, w3_words, w3_scales, offs, src, dst):
    xq = mxq(f64(xT)[:, unstriped(offs)], 0, "e4m3")
    y = unpack_fp4(w1_words, w1_scales).T @ xq
    e = unpack_fp4(w2_words, w2_scales).T @ xq
    h = unpack_fp4(w3_words, w3_scales).T @ xq
    return (np.tanh(y[:, unstriped(dst)] + e[:, unstriped(src)])) * h[:, unstriped(src)]

@@ -1,0 +1,199 @@
+from contextlib import ExitStack
+
+import concourse.mybir as mybir
+
+K, T, S, N, U = 1024, 2048, 1024, 128, 1024
+FLOPS = 3 * 2 * K * N * S
+
+F32 = mybir.dt.float32
+BF16 = mybir.dt.bfloat16
+U32 = mybir.dt.uint32
+I32 = mybir.dt.int32
+U16 = mybir.dt.uint16
+U8 = mybir.dt.uint8
+FP8X4 = mybir.dt.float8_e4m3fn_x4
+FP4X4 = mybir.dt.float4_e2m1fn_x4
+ACT = mybir.ActivationFunctionType
+ALU = mybir.AluOpType
+
+P = 128
+PASSES = K // 512
+LIST_ROWS = 16
+
+LOADS = (
+    ((1024, "sv"), (1024, "sv")),
+    ((1024, "sv"), (1024, "sv")),
+    ((512, "s"), (512, "s"), (512, "s"), (512, "s")),
+    ((512, "s"), (512, "s"), (512, "s"), (256, "v"), (256, "v")),
+)
+EDGE_PIECES = (512, 256, 256)
+
+
+def tile_picked_edgeatt_tanh_e_kernel(
+    tc, xT, w1_words, w1_scales, w2_words, w2_scales, w3_words, w3_scales, offs, src, dst, out
+):
+    nc = tc.nc
+    with ExitStack() as ctx:
+        keep = ctx.enter_context(tc.tile_pool(name="keep", bufs=1))
+        psum = ctx.enter_context(tc.psum_pool(name="psum", bufs=1))
+
+        offs_sb = keep.tile([P, S // LIST_ROWS], U16, name="offs_sb")
+        src_sb = keep.tile([P, U // LIST_ROWS], U16, name="src_sb")
+        dst_sb = keep.tile([P, U // LIST_ROWS], U16, name="dst_sb")
+
+        w_words = [keep.tile([P, PASSES, 2 * N], U8, name=f"w_words{i}", align_bytes=64) for i in range(3)]
+        w_scales = [keep.tile([P, PASSES, N], U8, name=f"w_scales{i}", align_bytes=64) for i in range(3)]
+        for i in range(3):
+            nc.gpsimd.memset(w_scales[i][:].bitcast(I32), 0)
+
+        def entries(list_sb, a, b):
+            return list_sb[:, a // LIST_ROWS : b // LIST_ROWS]
+
+        x_rows = xT.rearrange("(z p u e) t -> z u p e t", z=PASSES, p=P, u=2, e=2)
+        pairs = [keep.tile([P, T], U32, name=f"pairs{j}") for j in range(2 * PASSES)]
+        picked = [keep.tile([P, 2, S], U32, name=f"picked{z}") for z in range(PASSES)]
+        woven = [keep.tile([P, 4 * S], BF16, name=f"woven{z}", align_bytes=64) for z in range(PASSES)]
+        x_codes = [keep.tile([P, S], U32, name=f"x_codes{z}", align_bytes=64) for z in range(PASSES)]
+        x_scales = [keep.tile([P, S], U8, name=f"x_scales{z}", align_bytes=64) for z in range(PASSES)]
+
+        raw = {}
+        for j in range(2 * PASSES):
+            c0 = 0
+            for i, (width, who) in enumerate(LOADS[j]):
+                raw[j, i] = keep.tile([P, 2, width], F32, name=f"raw{j}_{i}")
+                nc.sync.dma_start(raw[j, i][:], x_rows[j // 2, j % 2, :, :, c0 : c0 + width])
+                if j == 0 and i == 0:
+                    nc.sync.dma_start(offs_sb[:], offs)
+                c0 = c0 + width
+
+        def load_weight(i, words, scales):
+            nc.sync.dma_start(w_words[i][:].bitcast(I32), words.rearrange("z p b -> p z b").bitcast(I32))
+            for q in range(4):
+                nc.sync.dma_start(
+                    w_scales[i][32 * q : 32 * q + 4].bitcast(I32),
+                    scales[:, 4 * q : 4 * q + 4, :].rearrange("z r c -> r z c").bitcast(I32),
+                )
+
+        load_weight(0, w1_words, w1_scales)
+        load_weight(1, w2_words, w2_scales)
+        nc.sync.dma_start(dst_sb[:], dst)
+        nc.sync.dma_start(src_sb[:], src)
+        load_weight(2, w3_words, w3_scales)
+
+        def round_pairs(j):
+            as_bf16 = pairs[j][:].bitcast(BF16).rearrange("p (t e) -> p t e", e=2)
+            c0 = 0
+            for i, (width, who) in enumerate(LOADS[j]):
+                share = width // len(who)
+                for s, engine in enumerate(who):
+                    in_ = raw[j, i][:, :, s * share : (s + 1) * share].rearrange("p e t -> p t e")
+                    to = as_bf16[:, c0 + s * share : c0 + (s + 1) * share, :]
+                    if engine == "s":
+                        nc.scalar.activation(to, in_, ACT.Copy)
+                    else:
+                        nc.vector.tensor_copy(to, in_)
+                c0 = c0 + width
+
+        def gather(j, a, b):
+            nc.vector.tensor_copy(picked[j // 2][:, j % 2, a:b], pairs[j][:].indirect(entries(offs_sb, a, b)))
+
+        def weave(z, a, b, engine):
+            in_ = picked[z][:, :, a:b].rearrange("p u n -> p n u")
+            to = woven[z][:, 4 * a : 4 * b]
+            if engine == "s":
+                nc.scalar.copy(to.bitcast(U32).rearrange("p (n u) -> p n u", u=2), in_)
+            else:
+                in_ = picked[z][:, :, a:b].bitcast(I32).rearrange("p u n -> p n u")
+                nc.vector.tensor_copy(to.bitcast(I32).rearrange("p (n u) -> p n u", u=2), in_)
+
+        def quantize(z, a, b):
+            nc.vector.quantize_mx(
+                out=x_codes[z][:, a:b].bitcast(FP8X4), scales=x_scales[z][:, a:b], in_=woven[z][:, 4 * a : 4 * b]
+            )
+
+        def product(acc, i, z, a, b):
+            nc.tensor.matmul_mx(
+                out=acc,
+                lhsT=w_words[i][:, z, :].bitcast(FP4X4),
+                lhsT_scale=w_scales[i][:, z, :],
+                rhs=x_codes[z][:, a:b].bitcast(FP8X4),
+                rhs_scale=x_scales[z][:, a:b],
+                start=(z == 0),
+                stop=(z == PASSES - 1),
+            )
+
+        round_pairs(0)
+        gather(0, 0, S)
+        round_pairs(1)
+        gather(1, 0, S)
+        weave(0, 0, S, "v")
+        quantize(0, 0, S)
+        round_pairs(2)
+        gather(2, 0, S)
+        round_pairs(3)
+
+        y_a = psum.tile([P, 512], F32, name="y_a")
+        y_b = psum.tile([P, 256], F32, name="y_b")
+        y_c = psum.tile([P, 128], F32, name="y_c")
+        y_d = psum.tile([P, 128], F32, name="y_d")
+        e_ps = [psum.tile([P, 512], F32, name=f"e_ps{i}") for i in range(2)]
+        h_ps = [psum.tile([P, 512], F32, name=f"h_ps{i}") for i in range(2)]
+        y_sb = keep.tile([P, S], F32, name="y_sb")
+        e_sb = keep.tile([P, S], F32, name="e_sb")
+        h_sb = keep.tile([P, S], F32, name="h_sb")
+
+        product(y_a[:], 0, 0, 0, 512)
+        product(y_c[:], 0, 0, 768, 896)
+        product(y_d[:], 0, 0, 896, 1024)
+        product(y_b[:, 0:128], 0, 0, 512, 640)
+        product(e_ps[0][:], 1, 0, 0, 512)
+        product(e_ps[1][:], 1, 0, 512, 1024)
+
+        gather(3, 0, 256)
+        weave(1, 0, 256, "s")
+        gather(3, 256, 512)
+        weave(1, 256, 512, "s")
+        gather(3, 512, 768)
+        weave(1, 512, 768, "s")
+        quantize(1, 0, 512)
+        product(y_a[:], 0, 1, 0, 512)
+        gather(3, 768, 1024)
+        weave(1, 768, 896, "s")
+        weave(1, 896, 1024, "s")
+        quantize(1, 512, 768)
+        product(y_b[:, 0:128], 0, 1, 512, 640)
+        product(y_b[:, 128:256], 0, 0, 640, 768)
+        product(y_b[:, 128:256], 0, 1, 640, 768)
+        quantize(1, 768, 896)
+        product(y_c[:], 0, 1, 768, 896)
+        quantize(1, 896, 1024)
+        product(y_d[:], 0, 1, 896, 1024)
+        nc.vector.tensor_copy(y_sb[:, 0:512], y_a[:])
+        nc.scalar.activation(y_sb[:, 512:768], y_b[:], ACT.Copy)
+        nc.scalar.activation(y_sb[:, 768:896], y_c[:], ACT.Copy)
+        nc.scalar.activation(y_sb[:, 896:1024], y_d[:], ACT.Copy)
+        for i in range(2):
+            product(e_ps[i][:], 1, 1, 512 * i, 512 * (i + 1))
+            nc.scalar.activation(e_sb[:, 512 * i : 512 * (i + 1)], e_ps[i][:], ACT.Copy)
+        for i in range(2):
+            product(h_ps[i][:], 2, 0, 512 * i, 512 * (i + 1))
+            product(h_ps[i][:], 2, 1, 512 * i, 512 * (i + 1))
+            nc.scalar.activation(h_sb[:, 512 * i : 512 * (i + 1)], h_ps[i][:], ACT.Copy)
+
+        bounds = []
+        a = 0
+        for width in EDGE_PIECES:
+            bounds.append((a, a + width))
+            a = a + width
+        y_dst = [keep.tile([P, b - a], F32, name=f"y_dst{a}") for a, b in bounds]
+        logit = [keep.tile([P, b - a], F32, name=f"logit{a}") for a, b in bounds]
+        gate = [keep.tile([P, b - a], F32, name=f"gate{a}") for a, b in bounds]
+        message = [keep.tile([P, b - a], F32, name=f"message{a}") for a, b in bounds]
+        for i, (a, b) in enumerate(bounds):
+            nc.vector.tensor_copy(y_dst[i][:], y_sb[:].indirect(entries(dst_sb, a, b)))
+        for i, (a, b) in enumerate(bounds):
+            nc.vector.tensor_tensor(logit[i][:], e_sb[:].indirect(entries(src_sb, a, b)), y_dst[i][:], ALU.add)
+            nc.scalar.activation(gate[i][:], logit[i][:], ACT.Tanh)
+        for i, (a, b) in enumerate(bounds):
+            nc.vector.tensor_tensor(message[i][:], h_sb[:].indirect(entries(src_sb, a, b)), gate[i][:], ALU.mult)
+            nc.sync.dma_start(out[:, a:b], message[i][:])

@@ -21,12 +21,12 @@ PASSES = K // 512
 LIST_ROWS = 16
 
 LOADS = (
-    ((1024, "sv"), (1024, "sv")),
-    ((1024, "sv"), (1024, "sv")),
+    ((1024, "s"), (1024, "vvvvvsss")),
+    ((1024, "s"), (1024, "vvvvvsss")),
     ((512, "s"), (512, "s"), (512, "s"), (512, "s")),
     ((512, "s"), (512, "s"), (512, "s"), (256, "v"), (256, "v")),
 )
-EDGE_PIECES = (512, 256, 256)
+EDGE_PIECES = (512, 384, 128)
 
 
 def tile_picked_edgeatt_tanh_e_kernel(
@@ -51,7 +51,9 @@ def tile_picked_edgeatt_tanh_e_kernel(
 
         x_rows = xT.rearrange("(z p u e) t -> z u p e t", z=PASSES, p=P, u=2, e=2)
         pairs = [keep.tile([P, T], U32, name=f"pairs{j}") for j in range(2 * PASSES)]
-        picked = [keep.tile([P, 2, S], U32, name=f"picked{z}") for z in range(PASSES)]
+        picked = keep.tile([P, 2, S], U32, name="picked")
+        picked1 = keep.tile([P, 2, S], U32, name="picked1")
+        late = [picked1[:, :, a : a + 256] for a in range(0, S, 256)]
         woven = [keep.tile([P, 4 * S], BF16, name=f"woven{z}", align_bytes=64) for z in range(PASSES)]
         x_codes = [keep.tile([P, S], U32, name=f"x_codes{z}", align_bytes=64) for z in range(PASSES)]
         x_scales = [keep.tile([P, S], U8, name=f"x_scales{z}", align_bytes=64) for z in range(PASSES)]
@@ -69,25 +71,27 @@ def tile_picked_edgeatt_tanh_e_kernel(
         def load_weight(i, words, scales):
             nc.sync.dma_start(w_words[i][:].bitcast(I32), words.rearrange("z p b -> p z b").bitcast(I32))
             for q in range(4):
-                nc.sync.dma_start(
+                nc.gpsimd.dma_start(
                     w_scales[i][32 * q : 32 * q + 4].bitcast(I32),
                     scales[:, 4 * q : 4 * q + 4, :].rearrange("z r c -> r z c").bitcast(I32),
                 )
 
         load_weight(0, w1_words, w1_scales)
         load_weight(1, w2_words, w2_scales)
+        load_weight(2, w3_words, w3_scales)
         nc.sync.dma_start(dst_sb[:], dst)
         nc.sync.dma_start(src_sb[:], src)
-        load_weight(2, w3_words, w3_scales)
 
         def round_pairs(j):
             as_bf16 = pairs[j][:].bitcast(BF16).rearrange("p (t e) -> p t e", e=2)
             c0 = 0
             for i, (width, who) in enumerate(LOADS[j]):
                 share = width // len(who)
-                for s, engine in enumerate(who):
-                    in_ = raw[j, i][:, :, s * share : (s + 1) * share].rearrange("p e t -> p t e")
-                    to = as_bf16[:, c0 + s * share : c0 + (s + 1) * share, :]
+                for engine in sorted(set(who)):
+                    lo = who.index(engine) * share
+                    hi = lo + len([c for c in who if c == engine]) * share
+                    in_ = raw[j, i][:, :, lo:hi].rearrange("p e t -> p t e")
+                    to = as_bf16[:, c0 + lo : c0 + hi, :]
                     if engine == "s":
                         nc.scalar.activation(to, in_, ACT.Copy)
                     else:
@@ -95,15 +99,16 @@ def tile_picked_edgeatt_tanh_e_kernel(
                 c0 = c0 + width
 
         def gather(j, a, b):
-            nc.vector.tensor_copy(picked[j // 2][:, j % 2, a:b], pairs[j][:].indirect(entries(offs_sb, a, b)))
+            to = picked[:, j, a:b] if j < 2 else picked1[:, j - 2, a:b]
+            nc.vector.tensor_copy(to, pairs[j][:].indirect(entries(offs_sb, a, b)))
 
         def weave(z, a, b, engine):
-            in_ = picked[z][:, :, a:b].rearrange("p u n -> p n u")
             to = woven[z][:, 4 * a : 4 * b]
             if engine == "s":
+                in_ = late[a // 256][:, :, a % 256 : a % 256 + b - a].rearrange("p u n -> p n u")
                 nc.scalar.copy(to.bitcast(U32).rearrange("p (n u) -> p n u", u=2), in_)
             else:
-                in_ = picked[z][:, :, a:b].bitcast(I32).rearrange("p u n -> p n u")
+                in_ = picked[:, :, a:b].bitcast(I32).rearrange("p u n -> p n u")
                 nc.vector.tensor_copy(to.bitcast(I32).rearrange("p (n u) -> p n u", u=2), in_)
 
         def quantize(z, a, b):
@@ -147,6 +152,8 @@ def tile_picked_edgeatt_tanh_e_kernel(
         product(y_d[:], 0, 0, 896, 1024)
         product(y_b[:, 0:128], 0, 0, 512, 640)
         product(e_ps[0][:], 1, 0, 0, 512)
+        product(h_ps[0][:], 2, 0, 0, 512)
+        product(h_ps[1][:], 2, 0, 512, 1024)
         product(e_ps[1][:], 1, 0, 512, 1024)
 
         gather(3, 0, 256)
@@ -172,28 +179,28 @@ def tile_picked_edgeatt_tanh_e_kernel(
         nc.scalar.activation(y_sb[:, 512:768], y_b[:], ACT.Copy)
         nc.scalar.activation(y_sb[:, 768:896], y_c[:], ACT.Copy)
         nc.scalar.activation(y_sb[:, 896:1024], y_d[:], ACT.Copy)
-        for i in range(2):
-            product(e_ps[i][:], 1, 1, 512 * i, 512 * (i + 1))
-            nc.scalar.activation(e_sb[:, 512 * i : 512 * (i + 1)], e_ps[i][:], ACT.Copy)
-        for i in range(2):
-            product(h_ps[i][:], 2, 0, 512 * i, 512 * (i + 1))
-            product(h_ps[i][:], 2, 1, 512 * i, 512 * (i + 1))
-            nc.scalar.activation(h_sb[:, 512 * i : 512 * (i + 1)], h_ps[i][:], ACT.Copy)
+        for acc, w, half, to in (
+            (e_ps[0], 1, 0, e_sb),
+            (h_ps[0], 2, 0, h_sb),
+            (h_ps[1], 2, 1, h_sb),
+            (e_ps[1], 1, 1, e_sb),
+        ):
+            product(acc[:], w, 1, 512 * half, 512 * (half + 1))
+            nc.scalar.activation(to[:, 512 * half : 512 * (half + 1)], acc[:], ACT.Copy)
 
-        bounds = []
+        halves = [(0, 512), (512, 1024)]
+        y_dst = [keep.tile([P, b - a], F32, name=f"y_dst{a}") for a, b in halves]
+        logit = [keep.tile([P, b - a], F32, name=f"logit{a}") for a, b in halves]
+        gate = keep.tile([P, U], F32, name="gate")
+        for i, (a, b) in enumerate(halves):
+            nc.vector.tensor_copy(y_dst[i][:], y_sb[:].indirect(entries(dst_sb, a, b)))
+        for i, (a, b) in enumerate(halves):
+            nc.vector.tensor_tensor(logit[i][:], e_sb[:].indirect(entries(src_sb, a, b)), y_dst[i][:], ALU.add)
+            nc.scalar.activation(gate[:, a:b], logit[i][:], ACT.Tanh)
         a = 0
         for width in EDGE_PIECES:
-            bounds.append((a, a + width))
-            a = a + width
-        y_dst = [keep.tile([P, b - a], F32, name=f"y_dst{a}") for a, b in bounds]
-        logit = [keep.tile([P, b - a], F32, name=f"logit{a}") for a, b in bounds]
-        gate = [keep.tile([P, b - a], F32, name=f"gate{a}") for a, b in bounds]
-        message = [keep.tile([P, b - a], F32, name=f"message{a}") for a, b in bounds]
-        for i, (a, b) in enumerate(bounds):
-            nc.vector.tensor_copy(y_dst[i][:], y_sb[:].indirect(entries(dst_sb, a, b)))
-        for i, (a, b) in enumerate(bounds):
-            nc.vector.tensor_tensor(logit[i][:], e_sb[:].indirect(entries(src_sb, a, b)), y_dst[i][:], ALU.add)
-            nc.scalar.activation(gate[i][:], logit[i][:], ACT.Tanh)
-        for i, (a, b) in enumerate(bounds):
-            nc.vector.tensor_tensor(message[i][:], h_sb[:].indirect(entries(src_sb, a, b)), gate[i][:], ALU.mult)
-            nc.sync.dma_start(out[:, a:b], message[i][:])
+            b = a + width
+            message = keep.tile([P, width], F32, name=f"message{a}")
+            nc.vector.tensor_tensor(message[:], h_sb[:].indirect(entries(src_sb, a, b)), gate[:, a:b], ALU.mult)
+            nc.sync.dma_start(out[:, a:b], message[:])
+            a = b

@@ -21,10 +21,10 @@ PASSES = K // 512
 LIST_ROWS = 16
 
 LOADS = (
+    (),
     ((1024, "s"), (1024, "vvvvvsss")),
-    ((1024, "s"), (1024, "vvvvvsss")),
-    ((512, "s"), (512, "s"), (512, "s"), (512, "s")),
-    ((512, "s"), (512, "s"), (512, "s"), (256, "v"), (256, "v")),
+    ((1024, "s"), (1024, "vvvvssss")),
+    ((1024, "s"), (768, "vvs"), (256, "v")),
 )
 EDGE_PIECES = (512, 384, 128)
 
@@ -44,37 +44,47 @@ def tile_picked_edgeatt_tanh_e_kernel(
         w_words = [keep.tile([P, PASSES, 2 * N], U8, name=f"w_words{i}", align_bytes=64) for i in range(3)]
         w_scales = [keep.tile([P, PASSES, N], U8, name=f"w_scales{i}", align_bytes=64) for i in range(3)]
         for i in range(3):
-            nc.gpsimd.memset(w_scales[i][:].bitcast(I32), 0)
+            nc.vector.memset(w_scales[i][:].bitcast(I32), 0)
+        scale_loads = [(i, scales, q) for i, scales in enumerate((w1_scales, w2_scales, w3_scales)) for q in range(4)]
+
+        def load_scales(first, last):
+            for i, scales, q in scale_loads[first:last]:
+                nc.sync.dma_start(
+                    w_scales[i][32 * q : 32 * q + 4].bitcast(I32),
+                    scales[:, 4 * q : 4 * q + 4, :].rearrange("z r c -> r z c").bitcast(I32),
+                )
 
         def entries(list_sb, a, b):
             return list_sb[:, a // LIST_ROWS : b // LIST_ROWS]
 
         x_rows = xT.rearrange("(z p u e) t -> z u p e t", z=PASSES, p=P, u=2, e=2)
-        pairs = [keep.tile([P, T], U32, name=f"pairs{j}") for j in range(2 * PASSES)]
-        picked = keep.tile([P, 2, S], U32, name="picked")
+        pairs = {j: keep.tile([P, T], U32, name=f"pairs{j}") for j in range(1, 2 * PASSES)}
         picked1 = keep.tile([P, 2, S], U32, name="picked1")
         late = [picked1[:, :, a : a + 256] for a in range(0, S, 256)]
         woven = [keep.tile([P, 4 * S], BF16, name=f"woven{z}", align_bytes=64) for z in range(PASSES)]
         x_codes = [keep.tile([P, S], U32, name=f"x_codes{z}", align_bytes=64) for z in range(PASSES)]
         x_scales = [keep.tile([P, S], U8, name=f"x_scales{z}", align_bytes=64) for z in range(PASSES)]
 
+        first_rows = [keep.tile([P, T], F32, name=f"first_row{e}") for e in range(2)]
+        for e in range(2):
+            nc.sync.dma_start(first_rows[e][:], x_rows[0, 0, :, e, :])
+            if e == 0:
+                nc.sync.dma_start(offs_sb[:], offs)
+        load_scales(0, 5)
         raw = {}
         for j in range(2 * PASSES):
             c0 = 0
             for i, (width, who) in enumerate(LOADS[j]):
                 raw[j, i] = keep.tile([P, 2, width], F32, name=f"raw{j}_{i}")
                 nc.sync.dma_start(raw[j, i][:], x_rows[j // 2, j % 2, :, :, c0 : c0 + width])
-                if j == 0 and i == 0:
-                    nc.sync.dma_start(offs_sb[:], offs)
+                if j == 1:
+                    load_scales(*((5, 6), (6, 11))[i])
+                if j == 2 and i == 0:
+                    load_scales(11, 12)
                 c0 = c0 + width
 
         def load_weight(i, words, scales):
             nc.sync.dma_start(w_words[i][:].bitcast(I32), words.rearrange("z p b -> p z b").bitcast(I32))
-            for q in range(4):
-                nc.gpsimd.dma_start(
-                    w_scales[i][32 * q : 32 * q + 4].bitcast(I32),
-                    scales[:, 4 * q : 4 * q + 4, :].rearrange("z r c -> r z c").bitcast(I32),
-                )
 
         load_weight(0, w1_words, w1_scales)
         load_weight(1, w2_words, w2_scales)
@@ -99,17 +109,16 @@ def tile_picked_edgeatt_tanh_e_kernel(
                 c0 = c0 + width
 
         def gather(j, a, b):
-            to = picked[:, j, a:b] if j < 2 else picked1[:, j - 2, a:b]
+            if j == 1:
+                to = woven[0][:].bitcast(U32).rearrange("p (n u) -> p n u", u=2)[:, a:b, 1]
+            else:
+                to = picked1[:, j - 2, a:b]
             nc.vector.tensor_copy(to, pairs[j][:].indirect(entries(offs_sb, a, b)))
 
         def weave(z, a, b, engine):
             to = woven[z][:, 4 * a : 4 * b]
-            if engine == "s":
-                in_ = late[a // 256][:, :, a % 256 : a % 256 + b - a].rearrange("p u n -> p n u")
-                nc.scalar.copy(to.bitcast(U32).rearrange("p (n u) -> p n u", u=2), in_)
-            else:
-                in_ = picked[:, :, a:b].bitcast(I32).rearrange("p u n -> p n u")
-                nc.vector.tensor_copy(to.bitcast(I32).rearrange("p (n u) -> p n u", u=2), in_)
+            in_ = late[a // 256][:, :, a % 256 : a % 256 + b - a].rearrange("p u n -> p n u")
+            nc.scalar.copy(to.bitcast(U32).rearrange("p (n u) -> p n u", u=2), in_)
 
         def quantize(z, a, b):
             nc.vector.quantize_mx(
@@ -127,11 +136,11 @@ def tile_picked_edgeatt_tanh_e_kernel(
                 stop=(z == PASSES - 1),
             )
 
-        round_pairs(0)
-        gather(0, 0, S)
+        for e in range(2):
+            to = woven[0][:].rearrange("p (n t) -> p n t", t=4)[:, :, e]
+            nc.vector.tensor_copy(to, first_rows[e][:].indirect(offs_sb[:]))
         round_pairs(1)
         gather(1, 0, S)
-        weave(0, 0, S, "v")
         quantize(0, 0, S)
         round_pairs(2)
         gather(2, 0, S)

@@ -21,10 +21,10 @@ PASSES = K // 512
 LIST_ROWS = 16
 
 LOADS = (
-    (),
     ((1024, "s"), (1024, "vvvvvsss")),
-    ((1024, "s"), (1024, "vvvvssss")),
-    ((1024, "s"), (768, "vvs"), (256, "v")),
+    ((1536, "vvvvvsss"), (512, "vvvs")),
+    ((768, "s"), (768, "s"), (512, "vsss")),
+    ((768, "s"), (640, "s"), (384, "v"), (256, "v")),
 )
 EDGE_PIECES = (512, 384, 128)
 
@@ -58,28 +58,29 @@ def tile_picked_edgeatt_tanh_e_kernel(
             return list_sb[:, a // LIST_ROWS : b // LIST_ROWS]
 
         x_rows = xT.rearrange("(z p u e) t -> z u p e t", z=PASSES, p=P, u=2, e=2)
-        pairs = {j: keep.tile([P, T], U32, name=f"pairs{j}") for j in range(1, 2 * PASSES)}
+        pairs = {j: keep.tile([P, T], U32, name=f"pairs{j}") for j in range(2 * PASSES)}
+        picked0 = keep.tile([P, 2, S], U32, name="picked0")
         picked1 = keep.tile([P, 2, S], U32, name="picked1")
         late = [picked1[:, :, a : a + 256] for a in range(0, S, 256)]
         woven = [keep.tile([P, 4 * S], BF16, name=f"woven{z}", align_bytes=64) for z in range(PASSES)]
         x_codes = [keep.tile([P, S], U32, name=f"x_codes{z}", align_bytes=64) for z in range(PASSES)]
         x_scales = [keep.tile([P, S], U8, name=f"x_scales{z}", align_bytes=64) for z in range(PASSES)]
 
-        first_rows = [keep.tile([P, T], F32, name=f"first_row{e}") for e in range(2)]
-        for e in range(2):
-            nc.sync.dma_start(first_rows[e][:], x_rows[0, 0, :, e, :])
-            if e == 0:
-                nc.sync.dma_start(offs_sb[:], offs)
-        load_scales(0, 5)
         raw = {}
         for j in range(2 * PASSES):
             c0 = 0
             for i, (width, who) in enumerate(LOADS[j]):
                 raw[j, i] = keep.tile([P, 2, width], F32, name=f"raw{j}_{i}")
                 nc.sync.dma_start(raw[j, i][:], x_rows[j // 2, j % 2, :, :, c0 : c0 + width])
-                if j == 1:
-                    load_scales(*((5, 6), (6, 11))[i])
+                if j == 0 and i == 0:
+                    nc.sync.dma_start(offs_sb[:], offs)
+                if j == 0 and i == 1:
+                    load_scales(0, 5)
+                if j == 1 and i == 0:
+                    load_scales(5, 6)
                 if j == 2 and i == 0:
+                    load_scales(6, 11)
+                if j == 2 and i == 2:
                     load_scales(11, 12)
                 c0 = c0 + width
 
@@ -109,10 +110,7 @@ def tile_picked_edgeatt_tanh_e_kernel(
                 c0 = c0 + width
 
         def gather(j, a, b):
-            if j == 1:
-                to = woven[0][:].bitcast(U32).rearrange("p (n u) -> p n u", u=2)[:, a:b, 1]
-            else:
-                to = picked1[:, j - 2, a:b]
+            to = picked0[:, j, a:b] if j < 2 else picked1[:, j - 2, a:b]
             nc.vector.tensor_copy(to, pairs[j][:].indirect(entries(offs_sb, a, b)))
 
         def weave(z, a, b, engine):
@@ -136,12 +134,18 @@ def tile_picked_edgeatt_tanh_e_kernel(
                 stop=(z == PASSES - 1),
             )
 
-        for e in range(2):
-            to = woven[0][:].rearrange("p (n t) -> p n t", t=4)[:, :, e]
-            nc.vector.tensor_copy(to, first_rows[e][:].indirect(offs_sb[:]))
+        round_pairs(0)
+        gather(0, 0, S)
         round_pairs(1)
-        gather(1, 0, S)
-        quantize(0, 0, S)
+        for a in (0, 512):
+            gather(1, a, a + 512)
+        for a in (0, 512):
+            nc.vector.tensor_copy(
+                woven[0][:, 4 * a : 4 * a + 2048].bitcast(I32).rearrange("p (n u) -> p n u", u=2),
+                picked0[:, :, a : a + 512].bitcast(I32).rearrange("p u n -> p n u"),
+            )
+        for a in (0, 512):
+            quantize(0, a, a + 512)
         round_pairs(2)
         gather(2, 0, S)
         round_pairs(3)

@@ -18,14 +18,20 @@ ALU = mybir.AluOpType
 
 P = 128
 PASSES = K // 512
+PAIRS = 2 * PASSES
 LIST_ROWS = 16
+BANK = 512
+HALVES = ((0, BANK), (BANK, 2 * BANK))
 
 LOADS = (
-    ((1024, "s"), (1024, "vvvvvsss")),
-    ((1536, "vvvvvsss"), (512, "vvvs")),
-    ((768, "s"), (768, "s"), (512, "vsss")),
-    ((768, "s"), (640, "s"), (384, "v"), (256, "v")),
+    ((1024, 384), (1024, 768)),
+    ((1536, 960), (512, 384)),
+    ((768, 0), (768, 0), (512, 128)),
+    ((768, 0), (640, 0), (384, 384), (256, 256)),
 )
+SCALE_LOADS_BEHIND = {(1, 0): 4, (2, 0): 2, (2, 2): 4, (3, 1): 2}
+PIECE = 256
+NARROW = 128
 EDGE_PIECES = (512, 384, 128)
 
 
@@ -41,82 +47,73 @@ def tile_picked_edgeatt_tanh_e_kernel(
         src_sb = keep.tile([P, U // LIST_ROWS], U16, name="src_sb")
         dst_sb = keep.tile([P, U // LIST_ROWS], U16, name="dst_sb")
 
+        def entries(list_sb, a, b):
+            return list_sb[:, a // LIST_ROWS : b // LIST_ROWS]
+
         w_words = [keep.tile([P, PASSES, 2 * N], U8, name=f"w_words{i}", align_bytes=64) for i in range(3)]
         w_scales = [keep.tile([P, PASSES, N], U8, name=f"w_scales{i}", align_bytes=64) for i in range(3)]
         for i in range(3):
             nc.vector.memset(w_scales[i][:].bitcast(I32), 0)
         scale_loads = [(i, scales, q) for i, scales in enumerate((w1_scales, w2_scales, w3_scales)) for q in range(4)]
 
-        def load_scales(first, last):
-            for i, scales, q in scale_loads[first:last]:
-                nc.sync.dma_start(
-                    w_scales[i][32 * q : 32 * q + 4].bitcast(I32),
-                    scales[:, 4 * q : 4 * q + 4, :].rearrange("z r c -> r z c").bitcast(I32),
-                )
-
-        def entries(list_sb, a, b):
-            return list_sb[:, a // LIST_ROWS : b // LIST_ROWS]
+        def load_scale_rows(i, scales, q):
+            nc.sync.dma_start(
+                w_scales[i][32 * q : 32 * q + 4].bitcast(I32),
+                scales[:, 4 * q : 4 * q + 4, :].rearrange("z r c -> r z c").bitcast(I32),
+            )
 
         x_rows = xT.rearrange("(z p u e) t -> z u p e t", z=PASSES, p=P, u=2, e=2)
-        pairs = {j: keep.tile([P, T], U32, name=f"pairs{j}") for j in range(2 * PASSES)}
-        picked0 = keep.tile([P, 2, S], U32, name="picked0")
-        picked1 = keep.tile([P, 2, S], U32, name="picked1")
-        late = [picked1[:, :, a : a + 256] for a in range(0, S, 256)]
+        pairs = [keep.tile([P, T], U32, name=f"pairs{j}") for j in range(PAIRS)]
+        picked = [keep.tile([P, 2, S], U32, name=f"picked{z}") for z in range(PASSES)]
         woven = [keep.tile([P, 4 * S], BF16, name=f"woven{z}", align_bytes=64) for z in range(PASSES)]
         x_codes = [keep.tile([P, S], U32, name=f"x_codes{z}", align_bytes=64) for z in range(PASSES)]
         x_scales = [keep.tile([P, S], U8, name=f"x_scales{z}", align_bytes=64) for z in range(PASSES)]
 
         raw = {}
-        for j in range(2 * PASSES):
+        first_pair = keep.tile([P, 2 * T], F32, name="first_pair")
+        run = x_rows[0, 0].rearrange("p e t -> p (e t)")
+        cut = LOADS[0][0][0]
+        nc.sync.dma_start(first_pair[:, 0 : T + cut], run[:, 0 : T + cut])
+        nc.sync.dma_start(offs_sb[:], offs)
+        nc.sync.dma_start(first_pair[:, T + cut :], run[:, T + cut :])
+        raw[0, 0] = first_pair[:].rearrange("p (e t) -> p e t", e=2)[:, :, 0:cut]
+        raw[0, 1] = first_pair[:].rearrange("p (e t) -> p e t", e=2)[:, :, cut:]
+        issued = 0
+        for j in range(1, PAIRS):
             c0 = 0
-            for i, (width, who) in enumerate(LOADS[j]):
+            for i, (width, on_vector) in enumerate(LOADS[j]):
                 raw[j, i] = keep.tile([P, 2, width], F32, name=f"raw{j}_{i}")
                 nc.sync.dma_start(raw[j, i][:], x_rows[j // 2, j % 2, :, :, c0 : c0 + width])
-                if j == 0 and i == 0:
-                    nc.sync.dma_start(offs_sb[:], offs)
-                if j == 0 and i == 1:
-                    load_scales(0, 5)
-                if j == 1 and i == 0:
-                    load_scales(5, 6)
-                if j == 2 and i == 0:
-                    load_scales(6, 11)
-                if j == 2 and i == 2:
-                    load_scales(11, 12)
+                count = SCALE_LOADS_BEHIND.get((j, i), 0)
+                for load in scale_loads[issued : issued + count]:
+                    load_scale_rows(*load)
+                issued = issued + count
                 c0 = c0 + width
 
-        def load_weight(i, words, scales):
+        for i, words in enumerate((w1_words, w2_words, w3_words)):
             nc.sync.dma_start(w_words[i][:].bitcast(I32), words.rearrange("z p b -> p z b").bitcast(I32))
-
-        load_weight(0, w1_words, w1_scales)
-        load_weight(1, w2_words, w2_scales)
-        load_weight(2, w3_words, w3_scales)
         nc.sync.dma_start(dst_sb[:], dst)
         nc.sync.dma_start(src_sb[:], src)
 
-        def round_pairs(j):
+        def round_pair(j):
             as_bf16 = pairs[j][:].bitcast(BF16).rearrange("p (t e) -> p t e", e=2)
             c0 = 0
-            for i, (width, who) in enumerate(LOADS[j]):
-                share = width // len(who)
-                for engine in sorted(set(who)):
-                    lo = who.index(engine) * share
-                    hi = lo + len([c for c in who if c == engine]) * share
-                    in_ = raw[j, i][:, :, lo:hi].rearrange("p e t -> p t e")
-                    to = as_bf16[:, c0 + lo : c0 + hi, :]
-                    if engine == "s":
-                        nc.scalar.activation(to, in_, ACT.Copy)
-                    else:
-                        nc.vector.tensor_copy(to, in_)
+            for i, (width, on_vector) in enumerate(LOADS[j]):
+                rows = raw[j, i][:, :, :].rearrange("p e t -> p t e")
+                if on_vector < width:
+                    nc.scalar.activation(as_bf16[:, c0 + on_vector : c0 + width, :], rows[:, on_vector:, :], ACT.Copy)
+                if on_vector > 0:
+                    nc.vector.tensor_copy(as_bf16[:, c0 : c0 + on_vector, :], rows[:, 0:on_vector, :])
                 c0 = c0 + width
 
         def gather(j, a, b):
-            to = picked0[:, j, a:b] if j < 2 else picked1[:, j - 2, a:b]
-            nc.vector.tensor_copy(to, pairs[j][:].indirect(entries(offs_sb, a, b)))
+            nc.vector.tensor_copy(picked[j // 2][:, j % 2, a:b], pairs[j][:].indirect(entries(offs_sb, a, b)))
 
-        def weave(z, a, b, engine):
-            to = woven[z][:, 4 * a : 4 * b]
-            in_ = late[a // 256][:, :, a % 256 : a % 256 + b - a].rearrange("p u n -> p n u")
-            nc.scalar.copy(to.bitcast(U32).rearrange("p (n u) -> p n u", u=2), in_)
+        def weave(copy, word, z, a, b):
+            copy(
+                woven[z][:, 4 * a : 4 * b].bitcast(word).rearrange("p (n u) -> p n u", u=2),
+                picked[z][:, :, a:b].bitcast(word).rearrange("p u n -> p n u"),
+            )
 
         def quantize(z, a, b):
             nc.vector.quantize_mx(
@@ -134,82 +131,72 @@ def tile_picked_edgeatt_tanh_e_kernel(
                 stop=(z == PASSES - 1),
             )
 
-        round_pairs(0)
+        round_pair(0)
         gather(0, 0, S)
-        round_pairs(1)
-        for a in (0, 512):
-            gather(1, a, a + 512)
-        for a in (0, 512):
-            nc.vector.tensor_copy(
-                woven[0][:, 4 * a : 4 * a + 2048].bitcast(I32).rearrange("p (n u) -> p n u", u=2),
-                picked0[:, :, a : a + 512].bitcast(I32).rearrange("p u n -> p n u"),
-            )
-        for a in (0, 512):
-            quantize(0, a, a + 512)
-        round_pairs(2)
+        round_pair(1)
+        for a, b in HALVES:
+            gather(1, a, b)
+        for a, b in HALVES:
+            weave(nc.vector.tensor_copy, I32, 0, a, b)
+        for a, b in HALVES:
+            quantize(0, a, b)
+        round_pair(2)
         gather(2, 0, S)
-        round_pairs(3)
+        round_pair(3)
 
-        y_a = psum.tile([P, 512], F32, name="y_a")
-        y_b = psum.tile([P, 256], F32, name="y_b")
-        y_c = psum.tile([P, 128], F32, name="y_c")
-        y_d = psum.tile([P, 128], F32, name="y_d")
-        e_ps = [psum.tile([P, 512], F32, name=f"e_ps{i}") for i in range(2)]
-        h_ps = [psum.tile([P, 512], F32, name=f"h_ps{i}") for i in range(2)]
+        n2, n3, n3b, n4 = BANK, BANK + NARROW, BANK + PIECE, S - NARROW
+        y_half = psum.tile([P, BANK], F32, name="y_half")
+        y_third = psum.tile([P, PIECE], F32, name="y_third")
+        y_next = psum.tile([P, NARROW], F32, name="y_next")
+        y_last = psum.tile([P, NARROW], F32, name="y_last")
+        e_ps = [psum.tile([P, BANK], F32, name=f"e_ps{i}") for i in range(2)]
+        h_ps = [psum.tile([P, BANK], F32, name=f"h_ps{i}") for i in range(2)]
         y_sb = keep.tile([P, S], F32, name="y_sb")
         e_sb = keep.tile([P, S], F32, name="e_sb")
         h_sb = keep.tile([P, S], F32, name="h_sb")
+        e_and_h = ((e_ps[0], 1, 0, e_sb), (h_ps[0], 2, 0, h_sb), (h_ps[1], 2, 1, h_sb), (e_ps[1], 1, 1, e_sb))
 
-        product(y_a[:], 0, 0, 0, 512)
-        product(y_c[:], 0, 0, 768, 896)
-        product(y_d[:], 0, 0, 896, 1024)
-        product(y_b[:, 0:128], 0, 0, 512, 640)
-        product(e_ps[0][:], 1, 0, 0, 512)
-        product(h_ps[0][:], 2, 0, 0, 512)
-        product(h_ps[1][:], 2, 0, 512, 1024)
-        product(e_ps[1][:], 1, 0, 512, 1024)
+        product(y_half[:], 0, 0, 0, n2)
+        product(y_next[:], 0, 0, n3b, n4)
+        product(y_last[:], 0, 0, n4, S)
+        product(y_third[:, 0:NARROW], 0, 0, n2, n3)
+        for acc, i, half, to in e_and_h:
+            product(acc[:], i, 0, *HALVES[half])
 
-        gather(3, 0, 256)
-        weave(1, 0, 256, "s")
-        gather(3, 256, 512)
-        weave(1, 256, 512, "s")
-        gather(3, 512, 768)
-        weave(1, 512, 768, "s")
-        quantize(1, 0, 512)
-        product(y_a[:], 0, 1, 0, 512)
-        gather(3, 768, 1024)
-        weave(1, 768, 896, "s")
-        weave(1, 896, 1024, "s")
-        quantize(1, 512, 768)
-        product(y_b[:, 0:128], 0, 1, 512, 640)
-        product(y_b[:, 128:256], 0, 0, 640, 768)
-        product(y_b[:, 128:256], 0, 1, 640, 768)
-        quantize(1, 768, 896)
-        product(y_c[:], 0, 1, 768, 896)
-        quantize(1, 896, 1024)
-        product(y_d[:], 0, 1, 896, 1024)
-        nc.vector.tensor_copy(y_sb[:, 0:512], y_a[:])
-        nc.scalar.activation(y_sb[:, 512:768], y_b[:], ACT.Copy)
-        nc.scalar.activation(y_sb[:, 768:896], y_c[:], ACT.Copy)
-        nc.scalar.activation(y_sb[:, 896:1024], y_d[:], ACT.Copy)
-        for acc, w, half, to in (
-            (e_ps[0], 1, 0, e_sb),
-            (h_ps[0], 2, 0, h_sb),
-            (h_ps[1], 2, 1, h_sb),
-            (e_ps[1], 1, 1, e_sb),
-        ):
-            product(acc[:], w, 1, 512 * half, 512 * (half + 1))
-            nc.scalar.activation(to[:, 512 * half : 512 * (half + 1)], acc[:], ACT.Copy)
+        for a in range(0, n3b, PIECE):
+            gather(3, a, a + PIECE)
+            weave(nc.scalar.copy, U32, 1, a, a + PIECE)
+        quantize(1, 0, n2)
+        product(y_half[:], 0, 1, 0, n2)
+        gather(3, n3b, S)
+        weave(nc.scalar.copy, U32, 1, n3b, n4)
+        weave(nc.scalar.copy, U32, 1, n4, S)
+        quantize(1, n2, n3b)
+        product(y_third[:, 0:NARROW], 0, 1, n2, n3)
+        for z in range(PASSES):
+            product(y_third[:, NARROW:PIECE], 0, z, n3, n3b)
+        quantize(1, n3b, n4)
+        product(y_next[:], 0, 1, n3b, n4)
+        quantize(1, n4, S)
+        product(y_last[:], 0, 1, n4, S)
 
-        halves = [(0, 512), (512, 1024)]
-        y_dst = [keep.tile([P, b - a], F32, name=f"y_dst{a}") for a, b in halves]
-        logit = [keep.tile([P, b - a], F32, name=f"logit{a}") for a, b in halves]
+        nc.vector.tensor_copy(y_sb[:, 0:n2], y_half[:])
+        nc.scalar.activation(y_sb[:, n2:n3b], y_third[:], ACT.Copy)
+        nc.scalar.activation(y_sb[:, n3b:n4], y_next[:], ACT.Copy)
+        nc.scalar.activation(y_sb[:, n4:S], y_last[:], ACT.Copy)
+        for acc, i, half, to in e_and_h:
+            a, b = HALVES[half]
+            product(acc[:], i, 1, a, b)
+            nc.scalar.activation(to[:, a:b], acc[:], ACT.Copy)
+
+        y_dst = [keep.tile([P, b - a], F32, name=f"y_dst{a}") for a, b in HALVES]
+        logit = [keep.tile([P, b - a], F32, name=f"logit{a}") for a, b in HALVES]
         gate = keep.tile([P, U], F32, name="gate")
-        for i, (a, b) in enumerate(halves):
-            nc.vector.tensor_copy(y_dst[i][:], y_sb[:].indirect(entries(dst_sb, a, b)))
-        for i, (a, b) in enumerate(halves):
-            nc.vector.tensor_tensor(logit[i][:], e_sb[:].indirect(entries(src_sb, a, b)), y_dst[i][:], ALU.add)
-            nc.scalar.activation(gate[:, a:b], logit[i][:], ACT.Tanh)
+        for half, (a, b) in enumerate(HALVES):
+            nc.vector.tensor_copy(y_dst[half][:], y_sb[:].indirect(entries(dst_sb, a, b)))
+        for half, (a, b) in enumerate(HALVES):
+            nc.vector.tensor_tensor(logit[half][:], e_sb[:].indirect(entries(src_sb, a, b)), y_dst[half][:], ALU.add)
+            nc.scalar.activation(gate[:, a:b], logit[half][:], ACT.Tanh)
         a = 0
         for width in EDGE_PIECES:
             b = a + width

@@ -29,7 +29,7 @@ LOADS = (
     ((768, 0), (768, 0), (512, 128)),
     ((768, 0), (640, 0), (384, 384), (256, 256)),
 )
-SCALE_LOADS_BEHIND = {(1, 0): 4, (2, 0): 2, (2, 2): 4, (3, 1): 2}
+SCALE_LOADS_BEHIND = {}
 PIECE = 256
 NARROW = 128
 EDGE_PIECES = (512, 384, 128)
@@ -54,7 +54,8 @@ def tile_picked_edgeatt_tanh_e_kernel(
         w_scales = [keep.tile([P, PASSES, N], U8, name=f"w_scales{i}", align_bytes=64) for i in range(3)]
         for i in range(3):
             nc.vector.memset(w_scales[i][:].bitcast(I32), 0)
-        scale_loads = [(i, scales, q) for i, scales in enumerate((w1_scales, w2_scales, w3_scales)) for q in range(4)]
+        weights = ((0, w1_words, w1_scales), (1, w2_words, w2_scales), (2, w3_words, w3_scales))
+        scale_loads = [(i, scales, q) for i, words, scales in weights for q in range(4)]
 
         def load_scale_rows(i, scales, q):
             nc.sync.dma_start(
@@ -66,7 +67,7 @@ def tile_picked_edgeatt_tanh_e_kernel(
         pairs = [keep.tile([P, T], U32, name=f"pairs{j}") for j in range(PAIRS)]
         picked = [keep.tile([P, 2, S], U32, name=f"picked{z}") for z in range(PASSES)]
         woven = [keep.tile([P, 4 * S], BF16, name=f"woven{z}", align_bytes=64) for z in range(PASSES)]
-        x_codes = [keep.tile([P, S], U32, name=f"x_codes{z}", align_bytes=64) for z in range(PASSES)]
+        x_codes = [keep.tile([P, S], U32, name=f"x_codes{z}", tag=f"x_codes{z}", align_bytes=64) for z in range(PASSES)]
         x_scales = [keep.tile([P, S], U8, name=f"x_scales{z}", align_bytes=64) for z in range(PASSES)]
 
         raw = {}
@@ -90,10 +91,13 @@ def tile_picked_edgeatt_tanh_e_kernel(
                 issued = issued + count
                 c0 = c0 + width
 
-        for i, words in enumerate((w1_words, w2_words, w3_words)):
+        for place, (i, words, scales) in enumerate(weights):
             nc.sync.dma_start(w_words[i][:].bitcast(I32), words.rearrange("z p b -> p z b").bitcast(I32))
-        nc.sync.dma_start(dst_sb[:], dst)
-        nc.sync.dma_start(src_sb[:], src)
+            if i == 1:
+                nc.sync.dma_start(dst_sb[:], dst)
+                nc.sync.dma_start(src_sb[:], src)
+            for load in scale_loads[max(issued, 4 * place) : 4 * place + 4]:
+                load_scale_rows(*load)
 
         def round_pair(j):
             as_bf16 = pairs[j][:].bitcast(BF16).rearrange("p (t e) -> p t e", e=2)
@@ -147,21 +151,20 @@ def tile_picked_edgeatt_tanh_e_kernel(
         n2, n3, n3b, n4 = BANK, BANK + NARROW, BANK + PIECE, S - NARROW
         y_half = psum.tile([P, BANK], F32, name="y_half")
         y_third = psum.tile([P, PIECE], F32, name="y_third")
-        y_next = psum.tile([P, NARROW], F32, name="y_next")
-        y_last = psum.tile([P, NARROW], F32, name="y_last")
+        y_next = psum.tile([P, NARROW], F32, name="y_next", tag="shared0")
+        y_last = psum.tile([P, NARROW], F32, name="y_last", tag="shared1")
         e_ps = [psum.tile([P, BANK], F32, name=f"e_ps{i}") for i in range(2)]
-        h_ps = [psum.tile([P, BANK], F32, name=f"h_ps{i}") for i in range(2)]
         y_sb = keep.tile([P, S], F32, name="y_sb")
         e_sb = keep.tile([P, S], F32, name="e_sb")
         h_sb = keep.tile([P, S], F32, name="h_sb")
-        e_and_h = ((e_ps[0], 1, 0, e_sb), (h_ps[0], 2, 0, h_sb), (h_ps[1], 2, 1, h_sb), (e_ps[1], 1, 1, e_sb))
+
 
         product(y_half[:], 0, 0, 0, n2)
+        product(y_third[:, 0:NARROW], 0, 0, n2, n3)
         product(y_next[:], 0, 0, n3b, n4)
         product(y_last[:], 0, 0, n4, S)
-        product(y_third[:, 0:NARROW], 0, 0, n2, n3)
-        for acc, i, half, to in e_and_h:
-            product(acc[:], i, 0, *HALVES[half])
+        for half in range(2):
+            product(e_ps[half][:], 1, 0, *HALVES[half])
 
         for a in range(0, n3b, PIECE):
             gather(3, a, a + PIECE)
@@ -184,14 +187,18 @@ def tile_picked_edgeatt_tanh_e_kernel(
         nc.scalar.activation(y_sb[:, n2:n3b], y_third[:], ACT.Copy)
         nc.scalar.activation(y_sb[:, n3b:n4], y_next[:], ACT.Copy)
         nc.scalar.activation(y_sb[:, n4:S], y_last[:], ACT.Copy)
-        for acc, i, half, to in e_and_h:
-            a, b = HALVES[half]
-            product(acc[:], i, 1, a, b)
-            nc.scalar.activation(to[:, a:b], acc[:], ACT.Copy)
+        for half, (a, b) in enumerate(HALVES):
+            product(e_ps[half][:], 1, 1, a, b)
+            nc.scalar.activation(e_sb[:, a:b], e_ps[half][:], ACT.Copy)
+        for half, (a, b) in enumerate(HALVES):
+            h_ps = psum.tile([P, BANK], F32, name=f"h_ps{half}", tag=f"shared{half}")
+            for z in range(PASSES):
+                product(h_ps[:], 2, z, a, b)
+            nc.scalar.activation(h_sb[:, a:b], h_ps[:], ACT.Copy)
 
         y_dst = [keep.tile([P, b - a], F32, name=f"y_dst{a}") for a, b in HALVES]
         logit = [keep.tile([P, b - a], F32, name=f"logit{a}") for a, b in HALVES]
-        gate = keep.tile([P, U], F32, name="gate")
+        gate = keep.tile([P, U], F32, name="gate", tag="x_codes1", align_bytes=64)
         for half, (a, b) in enumerate(HALVES):
             nc.vector.tensor_copy(y_dst[half][:], y_sb[:].indirect(entries(dst_sb, a, b)))
         for half, (a, b) in enumerate(HALVES):

@@ -29,7 +29,7 @@ LOADS = (
     ((768, 0), (768, 0), (512, 128)),
     ((768, 0), (640, 0), (384, 384), (256, 256)),
 )
-SCALE_LOADS_BEHIND = {}
+SCALE_LOADS_BEHIND = {(1, 0): 4, (2, 0): 2, (2, 2): 2}
 PIECE = 256
 NARROW = 128
 EDGE_PIECES = (512, 384, 128)
@@ -65,7 +65,7 @@ def tile_picked_edgeatt_tanh_e_kernel(
 
         x_rows = xT.rearrange("(z p u e) t -> z u p e t", z=PASSES, p=P, u=2, e=2)
         pairs = [keep.tile([P, T], U32, name=f"pairs{j}") for j in range(PAIRS)]
-        picked = [keep.tile([P, 2, S], U32, name=f"picked{z}") for z in range(PASSES)]
+        picked = [keep.tile([P, 2, S], U32, name=f"picked{z}", tag=f"picked{z}") for z in range(PASSES)]
         woven = [keep.tile([P, 4 * S], BF16, name=f"woven{z}", align_bytes=64) for z in range(PASSES)]
         x_codes = [keep.tile([P, S], U32, name=f"x_codes{z}", tag=f"x_codes{z}", align_bytes=64) for z in range(PASSES)]
         x_scales = [keep.tile([P, S], U8, name=f"x_scales{z}", align_bytes=64) for z in range(PASSES)]
@@ -91,13 +91,12 @@ def tile_picked_edgeatt_tanh_e_kernel(
                 issued = issued + count
                 c0 = c0 + width
 
-        for place, (i, words, scales) in enumerate(weights):
+        for i, words, scales in weights:
             nc.sync.dma_start(w_words[i][:].bitcast(I32), words.rearrange("z p b -> p z b").bitcast(I32))
-            if i == 1:
-                nc.sync.dma_start(dst_sb[:], dst)
-                nc.sync.dma_start(src_sb[:], src)
-            for load in scale_loads[max(issued, 4 * place) : 4 * place + 4]:
-                load_scale_rows(*load)
+        nc.sync.dma_start(dst_sb[:], dst)
+        for load in scale_loads[issued:]:
+            load_scale_rows(*load)
+        nc.sync.dma_start(src_sb[:], src)
 
         def round_pair(j):
             as_bf16 = pairs[j][:].bitcast(BF16).rearrange("p (t e) -> p t e", e=2)
@@ -148,50 +147,36 @@ def tile_picked_edgeatt_tanh_e_kernel(
         gather(2, 0, S)
         round_pair(3)
 
-        n2, n3, n3b, n4 = BANK, BANK + NARROW, BANK + PIECE, S - NARROW
-        y_half = psum.tile([P, BANK], F32, name="y_half")
-        y_third = psum.tile([P, PIECE], F32, name="y_third")
-        y_next = psum.tile([P, NARROW], F32, name="y_next", tag="shared0")
-        y_last = psum.tile([P, NARROW], F32, name="y_last", tag="shared1")
+        groups = [(0, BANK)] + [(a, a + NARROW) for a in range(BANK, S, NARROW)]
+        y_ps = [psum.tile([P, b - a], F32, name=f"y_ps{a}", tag=f"bank{g}") for g, (a, b) in enumerate(groups)]
         e_ps = [psum.tile([P, BANK], F32, name=f"e_ps{i}") for i in range(2)]
-        y_sb = keep.tile([P, S], F32, name="y_sb")
+        for g, (a, b) in enumerate(groups):
+            product(y_ps[g][:], 0, 0, a, b)
+        for half, (a, b) in enumerate(HALVES):
+            product(e_ps[half][:], 1, 0, a, b)
+
+        for a in range(0, S, PIECE):
+            gather(3, a, a + PIECE)
+        for a, b in ((0, 256), (256, 512), (512, 768), (768, 896), (896, 1024)):
+            weave(nc.scalar.copy, U32, 1, a, b)
+        for a, b in ((0, 512), (512, 768), (768, 896), (896, 1024)):
+            quantize(1, a, b)
+        for g, (a, b) in enumerate(groups):
+            product(y_ps[g][:], 0, 1, a, b)
+
+        y_sb = keep.tile([P, S], F32, name="y_sb", tag="picked1")
         e_sb = keep.tile([P, S], F32, name="e_sb")
         h_sb = keep.tile([P, S], F32, name="h_sb")
-
-
-        product(y_half[:], 0, 0, 0, n2)
-        product(y_third[:, 0:NARROW], 0, 0, n2, n3)
-        product(y_next[:], 0, 0, n3b, n4)
-        product(y_last[:], 0, 0, n4, S)
-        for half in range(2):
-            product(e_ps[half][:], 1, 0, *HALVES[half])
-
-        for a in range(0, n3b, PIECE):
-            gather(3, a, a + PIECE)
-            weave(nc.scalar.copy, U32, 1, a, a + PIECE)
-        quantize(1, 0, n2)
-        product(y_half[:], 0, 1, 0, n2)
-        gather(3, n3b, S)
-        weave(nc.scalar.copy, U32, 1, n3b, n4)
-        weave(nc.scalar.copy, U32, 1, n4, S)
-        quantize(1, n2, n3b)
-        product(y_third[:, 0:NARROW], 0, 1, n2, n3)
-        for z in range(PASSES):
-            product(y_third[:, NARROW:PIECE], 0, z, n3, n3b)
-        quantize(1, n3b, n4)
-        product(y_next[:], 0, 1, n3b, n4)
-        quantize(1, n4, S)
-        product(y_last[:], 0, 1, n4, S)
-
-        nc.vector.tensor_copy(y_sb[:, 0:n2], y_half[:])
-        nc.scalar.activation(y_sb[:, n2:n3b], y_third[:], ACT.Copy)
-        nc.scalar.activation(y_sb[:, n3b:n4], y_next[:], ACT.Copy)
-        nc.scalar.activation(y_sb[:, n4:S], y_last[:], ACT.Copy)
+        for g, (a, b) in enumerate(groups):
+            if g in (0, 3):
+                nc.scalar.activation(y_sb[:, a:b], y_ps[g][:], ACT.Copy)
+            else:
+                nc.vector.tensor_copy(y_sb[:, a:b], y_ps[g][:])
         for half, (a, b) in enumerate(HALVES):
             product(e_ps[half][:], 1, 1, a, b)
             nc.scalar.activation(e_sb[:, a:b], e_ps[half][:], ACT.Copy)
         for half, (a, b) in enumerate(HALVES):
-            h_ps = psum.tile([P, BANK], F32, name=f"h_ps{half}", tag=f"shared{half}")
+            h_ps = psum.tile([P, BANK], F32, name=f"h_ps{half}", tag=f"bank{3 + half}")
             for z in range(PASSES):
                 product(h_ps[:], 2, z, a, b)
             nc.scalar.activation(h_sb[:, a:b], h_ps[:], ACT.Copy)

@@ -25,14 +25,15 @@ HALVES = ((0, BANK), (BANK, 2 * BANK))
 
 LOADS = (
     ((1024, 384), (1024, 768)),
-    ((1536, 960), (512, 384)),
-    ((768, 0), (768, 0), (512, 128)),
-    ((768, 0), (640, 0), (384, 384), (256, 256)),
+    ((1024, 384), (768, 512), (256, 160)),
+    ((384, 0), (640, 0), (640, 0), (384, 192)),
+    ((640, 0), (640, 0), (384, 384), (256, 256), (128, 128)),
 )
-SCALE_LOADS_BEHIND = {(1, 0): 4, (2, 0): 2, (2, 2): 2}
+SCALE_LOADS_BEHIND = {(1, 0): 3, (2, 1): 3, (3, 0): 2}
 PIECE = 256
 NARROW = 128
-EDGE_PIECES = (512, 384, 128)
+EDGE_PIECES = (384, 384, 128, 128)
+EDGE_PARTS = ((0, 384), (384, 768), (768, 1024))
 
 
 def tile_picked_edgeatt_tanh_e_kernel(
@@ -83,7 +84,7 @@ def tile_picked_edgeatt_tanh_e_kernel(
         for j in range(1, PAIRS):
             c0 = 0
             for i, (width, on_vector) in enumerate(LOADS[j]):
-                raw[j, i] = keep.tile([P, 2, width], F32, name=f"raw{j}_{i}")
+                raw[j, i] = keep.tile([P, 2, width], F32, name=f"raw{j}_{i}", tag=f"raw{j}_{i}", align_bytes=64)
                 nc.sync.dma_start(raw[j, i][:], x_rows[j // 2, j % 2, :, :, c0 : c0 + width])
                 count = SCALE_LOADS_BEHIND.get((j, i), 0)
                 for load in scale_loads[issued : issued + count]:
@@ -93,9 +94,9 @@ def tile_picked_edgeatt_tanh_e_kernel(
 
         for i, words, scales in weights:
             nc.sync.dma_start(w_words[i][:].bitcast(I32), words.rearrange("z p b -> p z b").bitcast(I32))
-        nc.sync.dma_start(dst_sb[:], dst)
         for load in scale_loads[issued:]:
             load_scale_rows(*load)
+        nc.sync.dma_start(dst_sb[:], dst)
         nc.sync.dma_start(src_sb[:], src)
 
         def round_pair(j):
@@ -112,15 +113,17 @@ def tile_picked_edgeatt_tanh_e_kernel(
         def gather(j, a, b):
             nc.vector.tensor_copy(picked[j // 2][:, j % 2, a:b], pairs[j][:].indirect(entries(offs_sb, a, b)))
 
-        def weave(copy, word, z, a, b):
+        def weave(copy, word, z, a, b, into=None):
             copy(
-                woven[z][:, 4 * a : 4 * b].bitcast(word).rearrange("p (n u) -> p n u", u=2),
+                (woven[z][:, 4 * a : 4 * b] if into is None else into[:]).bitcast(word).rearrange("p (n u) -> p n u", u=2),
                 picked[z][:, :, a:b].bitcast(word).rearrange("p u n -> p n u"),
             )
 
-        def quantize(z, a, b):
+        def quantize(z, a, b, of=None):
             nc.vector.quantize_mx(
-                out=x_codes[z][:, a:b].bitcast(FP8X4), scales=x_scales[z][:, a:b], in_=woven[z][:, 4 * a : 4 * b]
+                out=x_codes[z][:, a:b].bitcast(FP8X4),
+                scales=x_scales[z][:, a:b],
+                in_=woven[z][:, 4 * a : 4 * b] if of is None else of[:],
             )
 
         def product(acc, i, z, a, b):
@@ -137,13 +140,16 @@ def tile_picked_edgeatt_tanh_e_kernel(
         round_pair(0)
         gather(0, 0, S)
         round_pair(1)
-        for a, b in HALVES:
+        for a, b in ((0, PIECE), (PIECE, BANK), (BANK, S)):
             gather(1, a, b)
-        for a, b in HALVES:
+        for a, b in ((PIECE, BANK), (BANK, S)):
             weave(nc.vector.tensor_copy, I32, 0, a, b)
-        for a, b in HALVES:
+        for a, b in ((PIECE, BANK), (BANK, S)):
             quantize(0, a, b)
         round_pair(2)
+        woven_first = keep.tile([P, 4 * PIECE], BF16, name="woven_first", tag="raw2_0", align_bytes=64)
+        weave(nc.scalar.copy, U32, 0, 0, PIECE, woven_first)
+        quantize(0, 0, PIECE, woven_first)
         gather(2, 0, S)
         round_pair(3)
 
@@ -154,6 +160,8 @@ def tile_picked_edgeatt_tanh_e_kernel(
             product(y_ps[g][:], 0, 0, a, b)
         for half, (a, b) in enumerate(HALVES):
             product(e_ps[half][:], 1, 0, a, b)
+        h_second = psum.tile([P, BANK], F32, name="h_second")
+        product(h_second[:], 2, 0, BANK, S)
 
         for a in range(0, S, PIECE):
             gather(3, a, a + PIECE)
@@ -175,20 +183,21 @@ def tile_picked_edgeatt_tanh_e_kernel(
         for half, (a, b) in enumerate(HALVES):
             product(e_ps[half][:], 1, 1, a, b)
             nc.scalar.activation(e_sb[:, a:b], e_ps[half][:], ACT.Copy)
-        for half, (a, b) in enumerate(HALVES):
-            h_ps = psum.tile([P, BANK], F32, name=f"h_ps{half}", tag=f"bank{3 + half}")
-            for z in range(PASSES):
-                product(h_ps[:], 2, z, a, b)
-            nc.scalar.activation(h_sb[:, a:b], h_ps[:], ACT.Copy)
+        product(h_second[:], 2, 1, BANK, S)
+        nc.scalar.activation(h_sb[:, BANK:S], h_second[:], ACT.Copy)
+        h_first = psum.tile([P, BANK], F32, name="h_first", tag="bank4")
+        for z in range(PASSES):
+            product(h_first[:], 2, z, 0, BANK)
+        nc.scalar.activation(h_sb[:, 0:BANK], h_first[:], ACT.Copy)
 
-        y_dst = [keep.tile([P, b - a], F32, name=f"y_dst{a}") for a, b in HALVES]
-        logit = [keep.tile([P, b - a], F32, name=f"logit{a}") for a, b in HALVES]
+        y_dst = keep.tile([P, U], F32, name="y_dst")
+        logit = keep.tile([P, U], F32, name="logit")
         gate = keep.tile([P, U], F32, name="gate", tag="x_codes1", align_bytes=64)
         for half, (a, b) in enumerate(HALVES):
-            nc.vector.tensor_copy(y_dst[half][:], y_sb[:].indirect(entries(dst_sb, a, b)))
-        for half, (a, b) in enumerate(HALVES):
-            nc.vector.tensor_tensor(logit[half][:], e_sb[:].indirect(entries(src_sb, a, b)), y_dst[half][:], ALU.add)
-            nc.scalar.activation(gate[:, a:b], logit[half][:], ACT.Tanh)
+            nc.vector.tensor_copy(y_dst[:, a:b], y_sb[:].indirect(entries(dst_sb, a, b)))
+        for a, b in EDGE_PARTS:
+            nc.vector.tensor_tensor(logit[:, a:b], e_sb[:].indirect(entries(src_sb, a, b)), y_dst[:, a:b], ALU.add)
+            nc.scalar.activation(gate[:, a:b], logit[:, a:b], ACT.Tanh)
         a = 0
         for width in EDGE_PIECES:
             b = a + width

@@ -24,12 +24,13 @@ BANK = 512
 HALVES = ((0, BANK), (BANK, 2 * BANK))
 
 LOADS = (
-    ((1024, 384), (1024, 768)),
-    ((1024, 384), (768, 512), (256, 160)),
-    ((384, 0), (640, 0), (640, 0), (384, 192)),
-    ((640, 0), (640, 0), (384, 384), (256, 256), (128, 128)),
+    ((1152, 704), (896, 560)),
+    ((768, 432), (768, 480), (512, 320)),
+    ((1024, 0), (1024, 768)),
+    ((768, 0), (896, 416), (384, 240)),
 )
-SCALE_LOADS_BEHIND = {(1, 0): 3, (2, 1): 3, (3, 0): 2}
+SCALE_LOADS_BEHIND = {(1, 0): 2, (2, 0): 3, (2, 1): 3}
+RUNS = 2
 PIECE = 256
 NARROW = 128
 EDGE_PIECES = (384, 384, 128, 128)
@@ -72,20 +73,22 @@ def tile_picked_edgeatt_tanh_e_kernel(
         x_scales = [keep.tile([P, S], U8, name=f"x_scales{z}", align_bytes=64) for z in range(PASSES)]
 
         raw = {}
-        first_pair = keep.tile([P, 2 * T], F32, name="first_pair")
-        run = x_rows[0, 0].rearrange("p e t -> p (e t)")
-        cut = LOADS[0][0][0]
-        nc.sync.dma_start(first_pair[:, 0 : T + cut], run[:, 0 : T + cut])
-        nc.sync.dma_start(offs_sb[:], offs)
-        nc.sync.dma_start(first_pair[:, T + cut :], run[:, T + cut :])
-        raw[0, 0] = first_pair[:].rearrange("p (e t) -> p e t", e=2)[:, :, 0:cut]
-        raw[0, 1] = first_pair[:].rearrange("p (e t) -> p e t", e=2)[:, :, cut:]
         issued = 0
-        for j in range(1, PAIRS):
+        for j in range(PAIRS):
             c0 = 0
+            if j < RUNS:
+                both = keep.tile([P, 2 * T], F32, name=f"both{j}")
+                run = x_rows[j // 2, j % 2].rearrange("p e t -> p (e t)")
             for i, (width, on_vector) in enumerate(LOADS[j]):
-                raw[j, i] = keep.tile([P, 2, width], F32, name=f"raw{j}_{i}", tag=f"raw{j}_{i}", align_bytes=64)
-                nc.sync.dma_start(raw[j, i][:], x_rows[j // 2, j % 2, :, :, c0 : c0 + width])
+                if j < RUNS:
+                    first = 0 if i == 0 else T + c0
+                    nc.sync.dma_start(both[:, first : T + c0 + width], run[:, first : T + c0 + width])
+                    raw[j, i] = both[:].rearrange("p (e t) -> p e t", e=2)[:, :, c0 : c0 + width]
+                else:
+                    raw[j, i] = keep.tile([P, 2, width], F32, name=f"raw{j}_{i}", tag=f"raw{j}_{i}", align_bytes=64)
+                    nc.sync.dma_start(raw[j, i][:], x_rows[j // 2, j % 2, :, :, c0 : c0 + width])
+                if (j, i) == (0, 0):
+                    nc.sync.dma_start(offs_sb[:], offs)
                 count = SCALE_LOADS_BEHIND.get((j, i), 0)
                 for load in scale_loads[issued : issued + count]:
                     load_scale_rows(*load)
@@ -142,15 +145,16 @@ def tile_picked_edgeatt_tanh_e_kernel(
         round_pair(1)
         for a, b in ((0, PIECE), (PIECE, BANK), (BANK, S)):
             gather(1, a, b)
-        for a, b in ((PIECE, BANK), (BANK, S)):
-            weave(nc.vector.tensor_copy, I32, 0, a, b)
-        for a, b in ((PIECE, BANK), (BANK, S)):
-            quantize(0, a, b)
+        for a in (0, PIECE):
+            weave(nc.scalar.copy, U32, 0, a, a + PIECE)
+        weave(nc.vector.tensor_copy, I32, 0, BANK, BANK + PIECE)
+        quantize(0, 0, BANK)
+        quantize(0, BANK, BANK + PIECE)
         round_pair(2)
-        woven_first = keep.tile([P, 4 * PIECE], BF16, name="woven_first", tag="raw2_0", align_bytes=64)
-        weave(nc.scalar.copy, U32, 0, 0, PIECE, woven_first)
-        quantize(0, 0, PIECE, woven_first)
+        woven_late = keep.tile([P, 4 * PIECE], BF16, name="woven_late", tag="raw2_1", align_bytes=64)
+        weave(nc.scalar.copy, U32, 0, BANK + PIECE, S, woven_late)
         gather(2, 0, S)
+        quantize(0, BANK + PIECE, S, woven_late)
         round_pair(3)
 
         groups = [(0, BANK)] + [(a, a + NARROW) for a in range(BANK, S, NARROW)]

@@ -29,7 +29,7 @@ LOADS = (
     ((1024, 0), (1024, 768)),
     ((768, 0), (896, 416), (384, 240)),
 )
-SCALE_LOADS_BEHIND = {(1, 0): 2, (2, 0): 3, (2, 1): 3}
+SCALE_LOADS_BEHIND = {(0, 1): 2, (1, 0): 2, (1, 2): 2, (2, 0): 3, (2, 1): 3}
 RUNS = 2
 PIECE = 256
 NARROW = 128

@@ -26,11 +26,11 @@ HALVES = ((0, BANK), (BANK, 2 * BANK))
 LOADS = (
     ((1152, 704), (896, 560)),
     ((768, 432), (768, 480), (512, 320)),
-    ((1024, 0), (1024, 768)),
-    ((768, 0), (896, 416), (384, 240)),
+    ((512, 0), (896, 576), (640, 400)),
+    ((512, 0), (896, 560), (640, 400)),
 )
-SCALE_LOADS_BEHIND = {(0, 1): 2, (1, 0): 2, (1, 2): 2, (2, 0): 3, (2, 1): 3}
-RUNS = 2
+SCALE_LOADS_BEHIND = {(0, 1): 3, (1, 0): 1, (1, 2): 3, (2, 0): 2, (3, 2): 3}
+RUNS = 4
 PIECE = 256
 NARROW = 128
 EDGE_PIECES = (384, 384, 128, 128)
@@ -77,7 +77,7 @@ def tile_picked_edgeatt_tanh_e_kernel(
         for j in range(PAIRS):
             c0 = 0
             if j < RUNS:
-                both = keep.tile([P, 2 * T], F32, name=f"both{j}")
+                both = keep.tile([P, 2 * T], F32, name=f"both{j}", tag=f"both{j}", align_bytes=64)
                 run = x_rows[j // 2, j % 2].rearrange("p e t -> p (e t)")
             for i, (width, on_vector) in enumerate(LOADS[j]):
                 if j < RUNS:
@@ -147,14 +147,12 @@ def tile_picked_edgeatt_tanh_e_kernel(
             gather(1, a, b)
         for a in (0, PIECE):
             weave(nc.scalar.copy, U32, 0, a, a + PIECE)
-        weave(nc.vector.tensor_copy, I32, 0, BANK, BANK + PIECE)
         quantize(0, 0, BANK)
-        quantize(0, BANK, BANK + PIECE)
         round_pair(2)
-        woven_late = keep.tile([P, 4 * PIECE], BF16, name="woven_late", tag="raw2_1", align_bytes=64)
-        weave(nc.scalar.copy, U32, 0, BANK + PIECE, S, woven_late)
+        woven_late = keep.tile([P, 4 * BANK], BF16, name="woven_late", tag="both2", align_bytes=64)
+        weave(nc.scalar.copy, U32, 0, BANK, S, woven_late)
         gather(2, 0, S)
-        quantize(0, BANK + PIECE, S, woven_late)
+        quantize(0, BANK, S, woven_late)
         round_pair(3)
 
         groups = [(0, BANK)] + [(a, a + NARROW) for a in range(BANK, S, NARROW)]

@@ -163,6 +163,15 @@ def tile_picked_edgeatt_tanh_e_kernel(
         for half, (a, b) in enumerate(HALVES):
             product(e_ps[half][:], 1, 0, a, b)
         h_second = psum.tile([P, BANK], F32, name="h_second")
+        nc.tensor.matmul_mx(
+            out=h_second[:],
+            lhsT=w_words[1][:, 0, :].bitcast(FP4X4),
+            lhsT_scale=w_scales[1][:, 0, :],
+            rhs=x_codes[0][:, 0:BANK].bitcast(FP8X4),
+            rhs_scale=x_scales[0][:, 0:BANK],
+            start=True,
+            stop=True,
+        )
         product(h_second[:], 2, 0, BANK, S)
 
         for a in range(0, S, PIECE):

@@ -18,19 +18,17 @@ ALU = mybir.AluOpType
 
 P = 128
 PASSES = K // 512
-PAIRS = 2 * PASSES
 LIST_ROWS = 16
 BANK = 512
 HALVES = ((0, BANK), (BANK, 2 * BANK))
 
 LOADS = (
-    ((1152, 704), (896, 560)),
-    ((768, 432), (768, 480), (512, 320)),
-    ((512, 0), (896, 576), (640, 400)),
-    ((512, 0), (896, 560), (640, 400)),
+    ((512, 0), (896, 608), (640, 400)),
+    ((768, 256), (768, 512), (512, 320)),
 )
-SCALE_LOADS_BEHIND = {(0, 1): 3, (1, 0): 1, (1, 2): 3, (2, 0): 2, (3, 2): 3}
-RUNS = 4
+SCALAR_PLACES = 640
+LATE = 768
+SCALE_LOADS_BEHIND = {("row", 3): 4, (0, 0): 2, (0, 2): 2, (1, 0): 3, (1, 2): 1}
 PIECE = 256
 NARROW = 128
 EDGE_PIECES = (384, 384, 128, 128)
@@ -57,48 +55,48 @@ def tile_picked_edgeatt_tanh_e_kernel(
         for i in range(3):
             nc.vector.memset(w_scales[i][:].bitcast(I32), 0)
         weights = ((0, w1_words, w1_scales), (1, w2_words, w2_scales), (2, w3_words, w3_scales))
-        scale_loads = [(i, scales, q) for i, words, scales in weights for q in range(4)]
+        scale_loads = [(i, q) for i in range(3) for q in range(4)]
 
-        def load_scale_rows(i, scales, q):
+        def load_scale_rows(i, q):
+            scales = weights[i][2]
             nc.sync.dma_start(
                 w_scales[i][32 * q : 32 * q + 4].bitcast(I32),
                 scales[:, 4 * q : 4 * q + 4, :].rearrange("z r c -> r z c").bitcast(I32),
             )
 
-        x_rows = xT.rearrange("(z p u e) t -> z u p e t", z=PASSES, p=P, u=2, e=2)
-        pairs = [keep.tile([P, T], U32, name=f"pairs{j}") for j in range(PAIRS)]
-        picked = [keep.tile([P, 2, S], U32, name=f"picked{z}", tag=f"picked{z}") for z in range(PASSES)]
+        x_rows = xT.rearrange("(z p t) n -> z p t n", z=PASSES, p=P, t=4)
+        rows = [keep.tile([P, T], F32, name=f"rows{t}") for t in range(4)]
+        singles = keep.tile([P, 4, S], F32, name="singles")
+        pairs = [keep.tile([P, T], U32, name=f"pairs{u}") for u in range(2)]
+        picked = keep.tile([P, 2, S], U32, name="picked", tag="picked")
         woven = [keep.tile([P, 4 * S], BF16, name=f"woven{z}", align_bytes=64) for z in range(PASSES)]
         x_codes = [keep.tile([P, S], U32, name=f"x_codes{z}", tag=f"x_codes{z}", align_bytes=64) for z in range(PASSES)]
         x_scales = [keep.tile([P, S], U8, name=f"x_scales{z}", align_bytes=64) for z in range(PASSES)]
 
+        def scale_loads_behind(key):
+            for load in scale_loads[: SCALE_LOADS_BEHIND.get(key, 0)]:
+                load_scale_rows(*load)
+                scale_loads.remove(load)
+
+        for t in range(4):
+            nc.sync.dma_start(rows[t][:], x_rows[0, :, t, :])
+            if t == 0:
+                nc.sync.dma_start(offs_sb[:], offs)
+            scale_loads_behind(("row", t))
         raw = {}
-        issued = 0
-        for j in range(PAIRS):
+        for u in range(2):
             c0 = 0
-            if j < RUNS:
-                both = keep.tile([P, 2 * T], F32, name=f"both{j}", tag=f"both{j}", align_bytes=64)
-                run = x_rows[j // 2, j % 2].rearrange("p e t -> p (e t)")
-            for i, (width, on_vector) in enumerate(LOADS[j]):
-                if j < RUNS:
-                    first = 0 if i == 0 else T + c0
-                    nc.sync.dma_start(both[:, first : T + c0 + width], run[:, first : T + c0 + width])
-                    raw[j, i] = both[:].rearrange("p (e t) -> p e t", e=2)[:, :, c0 : c0 + width]
-                else:
-                    raw[j, i] = keep.tile([P, 2, width], F32, name=f"raw{j}_{i}", tag=f"raw{j}_{i}", align_bytes=64)
-                    nc.sync.dma_start(raw[j, i][:], x_rows[j // 2, j % 2, :, :, c0 : c0 + width])
-                if (j, i) == (0, 0):
-                    nc.sync.dma_start(offs_sb[:], offs)
-                count = SCALE_LOADS_BEHIND.get((j, i), 0)
-                for load in scale_loads[issued : issued + count]:
-                    load_scale_rows(*load)
-                issued = issued + count
+            both = keep.tile([P, 2 * T], F32, name=f"both{u}", tag=f"both{u}", align_bytes=64)
+            run = x_rows[1, :, 2 * u : 2 * u + 2, :].rearrange("p e n -> p (e n)")
+            for i, (width, on_vector) in enumerate(LOADS[u]):
+                first = 0 if i == 0 else T + c0
+                nc.sync.dma_start(both[:, first : T + c0 + width], run[:, first : T + c0 + width])
+                raw[u, i] = both[:].rearrange("p (e n) -> p e n", e=2)[:, :, c0 : c0 + width]
+                scale_loads_behind((u, i))
                 c0 = c0 + width
 
         for i, words, scales in weights:
             nc.sync.dma_start(w_words[i][:].bitcast(I32), words.rearrange("z p b -> p z b").bitcast(I32))
-        for load in scale_loads[issued:]:
-            load_scale_rows(*load)
         nc.sync.dma_start(dst_sb[:], dst)
         nc.sync.dma_start(src_sb[:], src)
 
@@ -113,20 +111,31 @@ def tile_picked_edgeatt_tanh_e_kernel(
                     nc.vector.tensor_copy(as_bf16[:, c0 : c0 + on_vector, :], rows[:, 0:on_vector, :])
                 c0 = c0 + width
 
-        def gather(j, a, b):
-            nc.vector.tensor_copy(picked[j // 2][:, j % 2, a:b], pairs[j][:].indirect(entries(offs_sb, a, b)))
+        def gather_row(t, a, b):
+            nc.vector.tensor_copy(singles[:, t, a:b], rows[t][:].indirect(entries(offs_sb, a, b)))
 
-        def weave(copy, word, z, a, b, into=None):
-            copy(
-                (woven[z][:, 4 * a : 4 * b] if into is None else into[:]).bitcast(word).rearrange("p (n u) -> p n u", u=2),
-                picked[z][:, :, a:b].bitcast(word).rearrange("p u n -> p n u"),
+        def place(on_vector, u, a, b):
+            into = woven[0][:].rearrange("p (n t) -> p n t", t=4)[:, a:b, 2 * u : 2 * u + 2]
+            values = singles[:, 2 * u : 2 * u + 2, a:b].rearrange("p e n -> p n e")
+            if on_vector:
+                nc.vector.tensor_copy(into, values)
+            else:
+                nc.scalar.activation(into, values, ACT.Copy)
+
+        def gather(u, a, b):
+            nc.vector.tensor_copy(picked[:, u, a:b], pairs[u][:].indirect(entries(offs_sb, a, b)))
+
+        def weave(a, b):
+            nc.scalar.copy(
+                woven[1][:, 4 * a : 4 * b].bitcast(U32).rearrange("p (n u) -> p n u", u=2),
+                picked[:, :, a:b].rearrange("p u n -> p n u"),
             )
 
-        def quantize(z, a, b, of=None):
+        def quantize(z, a, b):
             nc.vector.quantize_mx(
                 out=x_codes[z][:, a:b].bitcast(FP8X4),
                 scales=x_scales[z][:, a:b],
-                in_=woven[z][:, 4 * a : 4 * b] if of is None else of[:],
+                in_=woven[z][:, 4 * a : 4 * b],
             )
 
         def product(acc, i, z, a, b):
@@ -140,20 +149,28 @@ def tile_picked_edgeatt_tanh_e_kernel(
                 stop=(z == PASSES - 1),
             )
 
-        round_pair(0)
-        gather(0, 0, S)
-        round_pair(1)
-        for a, b in ((0, PIECE), (PIECE, BANK), (BANK, S)):
-            gather(1, a, b)
-        for a in (0, PIECE):
-            weave(nc.scalar.copy, U32, 0, a, a + PIECE)
+        gather_row(0, 0, S)
+        for a, b in HALVES:
+            gather_row(1, a, b)
+            place(False, 0, a, min(b, LATE))
+        gather_row(2, 0, S)
+        for a in range(0, S, PIECE):
+            gather_row(3, a, a + PIECE)
+        for a, b in ((0, PIECE), (PIECE, BANK), (BANK, SCALAR_PLACES)):
+            place(False, 1, a, b)
+        place(True, 1, SCALAR_PLACES, LATE)
         quantize(0, 0, BANK)
-        round_pair(2)
-        woven_late = keep.tile([P, 4 * BANK], BF16, name="woven_late", tag="both2", align_bytes=64)
-        weave(nc.scalar.copy, U32, 0, BANK, S, woven_late)
-        gather(2, 0, S)
-        quantize(0, BANK, S, woven_late)
-        round_pair(3)
+        quantize(0, BANK, LATE)
+        round_pair(0)
+        woven_late = keep.tile([P, S - LATE, 4], BF16, name="woven_late", tag="both0", align_bytes=64)
+        nc.scalar.activation(woven_late[:], singles[:, :, LATE:S].rearrange("p t n -> p n t"), ACT.Copy)
+        gather(0, 0, S)
+        nc.vector.quantize_mx(
+            out=x_codes[0][:, LATE:S].bitcast(FP8X4),
+            scales=x_scales[0][:, LATE:S],
+            in_=woven_late[:].rearrange("p n t -> p (n t)"),
+        )
+        round_pair(1)
 
         groups = [(0, BANK)] + [(a, a + NARROW) for a in range(BANK, S, NARROW)]
         y_ps = [psum.tile([P, b - a], F32, name=f"y_ps{a}", tag=f"bank{g}") for g, (a, b) in enumerate(groups)]
@@ -175,15 +192,15 @@ def tile_picked_edgeatt_tanh_e_kernel(
         product(h_second[:], 2, 0, BANK, S)
 
         for a in range(0, S, PIECE):
-            gather(3, a, a + PIECE)
+            gather(1, a, a + PIECE)
         for a, b in ((0, 256), (256, 512), (512, 768), (768, 896), (896, 1024)):
-            weave(nc.scalar.copy, U32, 1, a, b)
+            weave(a, b)
         for a, b in ((0, 512), (512, 768), (768, 896), (896, 1024)):
             quantize(1, a, b)
         for g, (a, b) in enumerate(groups):
             product(y_ps[g][:], 0, 1, a, b)
 
-        y_sb = keep.tile([P, S], F32, name="y_sb", tag="picked1")
+        y_sb = keep.tile([P, S], F32, name="y_sb", tag="picked")
         e_sb = keep.tile([P, S], F32, name="e_sb")
         h_sb = keep.tile([P, S], F32, name="h_sb")
         for g, (a, b) in enumerate(groups):

@@ -28,7 +28,7 @@ LOADS = (
 )
 SCALAR_PLACES = 640
 LATE = 768
-SCALE_LOADS_BEHIND = {("row", 3): 4, (0, 0): 2, (0, 2): 2, (1, 0): 3, (1, 2): 1}
+SCALE_LOADS_BEHIND = {("row", 1): 4, ("row", 3): 4, (0, 2): 2, (1, 0): 2}
 PIECE = 256
 NARROW = 128
 EDGE_PIECES = (384, 384, 128, 128)
@@ -66,7 +66,8 @@ def tile_picked_edgeatt_tanh_e_kernel(
 
         x_rows = xT.rearrange("(z p t) n -> z p t n", z=PASSES, p=P, t=4)
         rows = [keep.tile([P, T], F32, name=f"rows{t}") for t in range(4)]
-        singles = keep.tile([P, 4, S], F32, name="singles")
+        singles = keep.tile([P, 4, S], BF16, name="singles")
+        row1_bf16 = keep.tile([P, T], BF16, name="row1_bf16")
         pairs = [keep.tile([P, T], U32, name=f"pairs{u}") for u in range(2)]
         picked = keep.tile([P, 2, S], U32, name="picked", tag="picked")
         woven = [keep.tile([P, 4 * S], BF16, name=f"woven{z}", align_bytes=64) for z in range(PASSES)]
@@ -150,9 +151,10 @@ def tile_picked_edgeatt_tanh_e_kernel(
             )
 
         gather_row(0, 0, S)
-        for a, b in HALVES:
-            gather_row(1, a, b)
-            place(False, 0, a, min(b, LATE))
+        nc.scalar.activation(row1_bf16[:], rows[1][:], ACT.Copy)
+        nc.scalar.activation(singles[:, 1, LATE:S], row1_bf16[:].indirect(entries(offs_sb, LATE, S)), ACT.Copy)
+        gather_row(1, 0, LATE)
+        place(False, 0, 0, LATE)
         gather_row(2, 0, S)
         for a in range(0, S, PIECE):
             gather_row(3, a, a + PIECE)
@@ -172,48 +174,54 @@ def tile_picked_edgeatt_tanh_e_kernel(
         )
         round_pair(1)
 
-        groups = [(0, BANK)] + [(a, a + NARROW) for a in range(BANK, S, NARROW)]
-        y_ps = [psum.tile([P, b - a], F32, name=f"y_ps{a}", tag=f"bank{g}") for g, (a, b) in enumerate(groups)]
-        e_ps = [psum.tile([P, BANK], F32, name=f"e_ps{i}") for i in range(2)]
-        for g, (a, b) in enumerate(groups):
-            product(y_ps[g][:], 0, 0, a, b)
-        for half, (a, b) in enumerate(HALVES):
-            product(e_ps[half][:], 1, 0, a, b)
+        banks = [(0, PIECE), (PIECE, BANK)] + [(a, a + NARROW) for a in range(BANK, S, NARROW)]
+        y_ps = [psum.tile([P, b - a], F32, name=f"y_ps{a}", tag=f"bank{g}") for g, (a, b) in enumerate(banks)]
+        for g, (a, b) in enumerate(banks):
+            product(y_ps[g][:, 0:NARROW], 0, 0, a, a + NARROW)
+        e_second = psum.tile([P, BANK], F32, name="e_second")
         h_second = psum.tile([P, BANK], F32, name="h_second")
-        nc.tensor.matmul_mx(
-            out=h_second[:],
-            lhsT=w_words[1][:, 0, :].bitcast(FP4X4),
-            lhsT_scale=w_scales[1][:, 0, :],
-            rhs=x_codes[0][:, 0:BANK].bitcast(FP8X4),
-            rhs_scale=x_scales[0][:, 0:BANK],
-            start=True,
-            stop=True,
-        )
+        product(e_second[:], 1, 0, BANK, S)
+        for a, b in HALVES:
+            nc.tensor.matmul_mx(
+                out=h_second[:],
+                lhsT=w_words[1][:, 0, :].bitcast(FP4X4),
+                lhsT_scale=w_scales[1][:, 0, :],
+                rhs=x_codes[0][:, a:b].bitcast(FP8X4),
+                rhs_scale=x_scales[0][:, a:b],
+                start=True,
+                stop=True,
+            )
         product(h_second[:], 2, 0, BANK, S)
 
         for a in range(0, S, PIECE):
             gather(1, a, a + PIECE)
         for a, b in ((0, 256), (256, 512), (512, 768), (768, 896), (896, 1024)):
             weave(a, b)
-        for a, b in ((0, 512), (512, 768), (768, 896), (896, 1024)):
+        for a, b in ((0, 256), (256, 512), (512, 768), (768, 896), (896, 1024)):
             quantize(1, a, b)
-        for g, (a, b) in enumerate(groups):
-            product(y_ps[g][:], 0, 1, a, b)
+        for g, (a, b) in enumerate(banks):
+            product(y_ps[g][:, 0:NARROW], 0, 1, a, a + NARROW)
+            if b - a > NARROW:
+                for z in range(PASSES):
+                    product(y_ps[g][:, NARROW:], 0, z, a + NARROW, b)
 
         y_sb = keep.tile([P, S], F32, name="y_sb", tag="picked")
         e_sb = keep.tile([P, S], F32, name="e_sb")
         h_sb = keep.tile([P, S], F32, name="h_sb")
-        for g, (a, b) in enumerate(groups):
-            if g in (0, 3):
+        for g, (a, b) in enumerate(banks):
+            if g in (0, 1, 5):
                 nc.scalar.activation(y_sb[:, a:b], y_ps[g][:], ACT.Copy)
             else:
                 nc.vector.tensor_copy(y_sb[:, a:b], y_ps[g][:])
-        for half, (a, b) in enumerate(HALVES):
-            product(e_ps[half][:], 1, 1, a, b)
-            nc.scalar.activation(e_sb[:, a:b], e_ps[half][:], ACT.Copy)
+        product(e_second[:], 1, 1, BANK, S)
+        nc.scalar.activation(e_sb[:, BANK:S], e_second[:], ACT.Copy)
+        e_first = psum.tile([P, BANK], F32, name="e_first", tag="bank4")
+        for z in range(PASSES):
+            product(e_first[:], 1, z, 0, BANK)
+        nc.scalar.activation(e_sb[:, 0:BANK], e_first[:], ACT.Copy)
         product(h_second[:], 2, 1, BANK, S)
         nc.scalar.activation(h_sb[:, BANK:S], h_second[:], ACT.Copy)
-        h_first = psum.tile([P, BANK], F32, name="h_first", tag="bank4")
+        h_first = psum.tile([P, BANK], F32, name="h_first", tag="bank5")
         for z in range(PASSES):
             product(h_first[:], 2, z, 0, BANK)
         nc.scalar.activation(h_sb[:, 0:BANK], h_first[:], ACT.Copy)

@@ -28,7 +28,7 @@ LOADS = (
 )
 SCALAR_PLACES = 640
 LATE = 768
-SCALE_LOADS_BEHIND = {("row", 1): 4, ("row", 3): 4, (0, 2): 2, (1, 0): 2}
+SCALE_LOADS_BEHIND = {(0, 2): 4}
 PIECE = 256
 NARROW = 128
 EDGE_PIECES = (384, 384, 128, 128)
@@ -55,7 +55,7 @@ def tile_picked_edgeatt_tanh_e_kernel(
         for i in range(3):
             nc.vector.memset(w_scales[i][:].bitcast(I32), 0)
         weights = ((0, w1_words, w1_scales), (1, w2_words, w2_scales), (2, w3_words, w3_scales))
-        scale_loads = [(i, q) for i in range(3) for q in range(4)]
+        scale_loads = [(1, q) for q in range(4)]
 
         def load_scale_rows(i, q):
             scales = weights[i][2]
@@ -96,9 +96,17 @@ def tile_picked_edgeatt_tanh_e_kernel(
                 scale_loads_behind((u, i))
                 c0 = c0 + width
 
-        for i, words, scales in weights:
-            nc.sync.dma_start(w_words[i][:].bitcast(I32), words.rearrange("z p b -> p z b").bitcast(I32))
+        def load_words(i):
+            nc.sync.dma_start(w_words[i][:].bitcast(I32), weights[i][1].rearrange("z p b -> p z b").bitcast(I32))
+
+        load_words(0)
+        for q in range(4):
+            load_scale_rows(0, q)
+        load_words(1)
         nc.sync.dma_start(dst_sb[:], dst)
+        load_words(2)
+        for q in range(4):
+            load_scale_rows(2, q)
         nc.sync.dma_start(src_sb[:], src)
 
         def round_pair(j):
@@ -180,17 +188,17 @@ def tile_picked_edgeatt_tanh_e_kernel(
             product(y_ps[g][:, 0:NARROW], 0, 0, a, a + NARROW)
         e_second = psum.tile([P, BANK], F32, name="e_second")
         h_second = psum.tile([P, BANK], F32, name="h_second")
-        product(e_second[:], 1, 0, BANK, S)
         for a, b in HALVES:
             nc.tensor.matmul_mx(
                 out=h_second[:],
-                lhsT=w_words[1][:, 0, :].bitcast(FP4X4),
-                lhsT_scale=w_scales[1][:, 0, :],
+                lhsT=w_words[0][:, 0, :].bitcast(FP4X4),
+                lhsT_scale=w_scales[0][:, 0, :],
                 rhs=x_codes[0][:, a:b].bitcast(FP8X4),
                 rhs_scale=x_scales[0][:, a:b],
                 start=True,
                 stop=True,
             )
+        product(e_second[:], 1, 0, BANK, S)
         product(h_second[:], 2, 0, BANK, S)
 
         for a in range(0, S, PIECE):

@@ -18,21 +18,13 @@ ALU = mybir.AluOpType
 
 P = 128
 PASSES = K // 512
+ROWS = 4 * PASSES
 LIST_ROWS = 16
 BANK = 512
-HALVES = ((0, BANK), (BANK, 2 * BANK))
-
-LOADS = (
-    ((512, 0), (896, 608), (640, 400)),
-    ((768, 256), (768, 512), (512, 320)),
-)
-SCALAR_PLACES = 640
-LATE = 768
-SCALE_LOADS_BEHIND = {(0, 2): 4}
 PIECE = 256
 NARROW = 128
-EDGE_PIECES = (384, 384, 128, 128)
-EDGE_PARTS = ((0, 384), (384, 768), (768, 1024))
+ON_VECTOR = (384, 384, 384, 512, 256, 256, 256)
+SUMS = (((256, 512), (0, 256)), ((512, 768), (768, 896)), ((896, 1024),))
 
 
 def tile_picked_edgeatt_tanh_e_kernel(
@@ -51,94 +43,56 @@ def tile_picked_edgeatt_tanh_e_kernel(
             return list_sb[:, a // LIST_ROWS : b // LIST_ROWS]
 
         w_words = [keep.tile([P, PASSES, 2 * N], U8, name=f"w_words{i}", align_bytes=64) for i in range(3)]
-        w_scales = [keep.tile([P, PASSES, N], U8, name=f"w_scales{i}", align_bytes=64) for i in range(3)]
-        for i in range(3):
-            nc.vector.memset(w_scales[i][:].bitcast(I32), 0)
-        weights = ((0, w1_words, w1_scales), (1, w2_words, w2_scales), (2, w3_words, w3_scales))
-        scale_loads = [(1, q) for q in range(4)]
+        w_scales = keep.tile([P, 3, PASSES, N], U8, name="w_scales", align_bytes=64)
+        nc.gpsimd.memset(w_scales[:].rearrange("p i z c -> p (i z c)").bitcast(I32), 0)
+        weights = ((w1_words, w1_scales), (w2_words, w2_scales), (w3_words, w3_scales))
 
-        def load_scale_rows(i, q):
-            scales = weights[i][2]
-            nc.sync.dma_start(
-                w_scales[i][32 * q : 32 * q + 4].bitcast(I32),
-                scales[:, 4 * q : 4 * q + 4, :].rearrange("z r c -> r z c").bitcast(I32),
-            )
+        def load_scale_rows(i, quadrants):
+            for q in quadrants:
+                nc.sync.dma_start(
+                    w_scales[32 * q : 32 * q + 4, i].bitcast(I32),
+                    weights[i][1][:, 4 * q : 4 * q + 4, :].rearrange("z r c -> r z c").bitcast(I32),
+                )
 
-        x_rows = xT.rearrange("(z p t) n -> z p t n", z=PASSES, p=P, t=4)
-        rows = [keep.tile([P, T], F32, name=f"rows{t}") for t in range(4)]
-        singles = keep.tile([P, 4, S], BF16, name="singles")
-        row1_bf16 = keep.tile([P, T], BF16, name="row1_bf16")
-        pairs = [keep.tile([P, T], U32, name=f"pairs{u}") for u in range(2)]
-        picked = keep.tile([P, 2, S], U32, name="picked", tag="picked")
-        woven = [keep.tile([P, 4 * S], BF16, name=f"woven{z}", align_bytes=64) for z in range(PASSES)]
+        def load_words(i):
+            nc.sync.dma_start(w_words[i][:].bitcast(I32), weights[i][0].rearrange("z p b -> p z b").bitcast(I32))
+
+
+        x_rows = xT.rearrange("(z p t) n -> z t p n", z=PASSES, p=P, t=4)
+        rows = [keep.tile([P, T], F32, name=f"rows{j}") for j in range(ROWS)]
+        picked = [keep.tile([P, 2, S], BF16, name=f"picked{u}") for u in range(ROWS // 2)]
+        woven = [keep.tile([P, 4 * S], BF16, name=f"woven{z}", tag=f"woven{z}", align_bytes=64) for z in range(PASSES)]
         x_codes = [keep.tile([P, S], U32, name=f"x_codes{z}", tag=f"x_codes{z}", align_bytes=64) for z in range(PASSES)]
         x_scales = [keep.tile([P, S], U8, name=f"x_scales{z}", align_bytes=64) for z in range(PASSES)]
 
-        def scale_loads_behind(key):
-            for load in scale_loads[: SCALE_LOADS_BEHIND.get(key, 0)]:
-                load_scale_rows(*load)
-                scale_loads.remove(load)
-
-        for t in range(4):
-            nc.sync.dma_start(rows[t][:], x_rows[0, :, t, :])
-            if t == 0:
+        for j in range(ROWS):
+            if j == ROWS - 1:
+                load_words(0)
+                load_words(1)
+            nc.sync.dma_start(rows[j][:], x_rows[j // 4, j % 4])
+            if j == 0:
                 nc.sync.dma_start(offs_sb[:], offs)
-            scale_loads_behind(("row", t))
-        raw = {}
-        for u in range(2):
-            c0 = 0
-            both = keep.tile([P, 2 * T], F32, name=f"both{u}", tag=f"both{u}", align_bytes=64)
-            run = x_rows[1, :, 2 * u : 2 * u + 2, :].rearrange("p e n -> p (e n)")
-            for i, (width, on_vector) in enumerate(LOADS[u]):
-                first = 0 if i == 0 else T + c0
-                nc.sync.dma_start(both[:, first : T + c0 + width], run[:, first : T + c0 + width])
-                raw[u, i] = both[:].rearrange("p (e n) -> p e n", e=2)[:, :, c0 : c0 + width]
-                scale_loads_behind((u, i))
-                c0 = c0 + width
-
-        def load_words(i):
-            nc.sync.dma_start(w_words[i][:].bitcast(I32), weights[i][1].rearrange("z p b -> p z b").bitcast(I32))
-
-        load_words(0)
-        for q in range(4):
-            load_scale_rows(0, q)
-        load_words(1)
-        nc.sync.dma_start(dst_sb[:], dst)
+            if 1 <= j <= 6:
+                load_scale_rows((j - 1) // 2, range(2 * ((j - 1) % 2), 2 * ((j - 1) % 2) + 2))
         load_words(2)
-        for q in range(4):
-            load_scale_rows(2, q)
+        nc.sync.dma_start(dst_sb[:], dst)
         nc.sync.dma_start(src_sb[:], src)
 
-        def round_pair(j):
-            as_bf16 = pairs[j][:].bitcast(BF16).rearrange("p (t e) -> p t e", e=2)
-            c0 = 0
-            for i, (width, on_vector) in enumerate(LOADS[j]):
-                rows = raw[j, i][:, :, :].rearrange("p e t -> p t e")
-                if on_vector < width:
-                    nc.scalar.activation(as_bf16[:, c0 + on_vector : c0 + width, :], rows[:, on_vector:, :], ACT.Copy)
-                if on_vector > 0:
-                    nc.vector.tensor_copy(as_bf16[:, c0 : c0 + on_vector, :], rows[:, 0:on_vector, :])
-                c0 = c0 + width
-
-        def gather_row(t, a, b):
-            nc.vector.tensor_copy(singles[:, t, a:b], rows[t][:].indirect(entries(offs_sb, a, b)))
-
-        def place(on_vector, u, a, b):
-            into = woven[0][:].rearrange("p (n t) -> p n t", t=4)[:, a:b, 2 * u : 2 * u + 2]
-            values = singles[:, 2 * u : 2 * u + 2, a:b].rearrange("p e n -> p n e")
+        def gather_row(on_vector, j, a, b):
+            into = picked[j // 2][:, j % 2, a:b]
+            values = rows[j][:].indirect(entries(offs_sb, a, b))
             if on_vector:
                 nc.vector.tensor_copy(into, values)
             else:
                 nc.scalar.activation(into, values, ACT.Copy)
 
-        def gather(u, a, b):
-            nc.vector.tensor_copy(picked[:, u, a:b], pairs[u][:].indirect(entries(offs_sb, a, b)))
-
-        def weave(a, b):
-            nc.scalar.copy(
-                woven[1][:, 4 * a : 4 * b].bitcast(U32).rearrange("p (n u) -> p n u", u=2),
-                picked[:, :, a:b].rearrange("p u n -> p n u"),
-            )
+        def place(u, a, b, on_vector=True):
+            into = woven[u // 2][:].rearrange("p (n t) -> p n t", t=4)[:, a:b, 2 * (u % 2) : 2 * (u % 2) + 2]
+            values = picked[u][:, :, a:b].rearrange("p e n -> p n e")
+            if on_vector:
+                nc.vector.tensor_copy(into, values)
+            else:
+                nc.scalar.activation(into, values, ACT.Copy)
 
         def quantize(z, a, b):
             nc.vector.quantize_mx(
@@ -147,105 +101,88 @@ def tile_picked_edgeatt_tanh_e_kernel(
                 in_=woven[z][:, 4 * a : 4 * b],
             )
 
-        def product(acc, i, z, a, b):
+        def product(acc, i, z, a, b, start, stop):
             nc.tensor.matmul_mx(
                 out=acc,
                 lhsT=w_words[i][:, z, :].bitcast(FP4X4),
-                lhsT_scale=w_scales[i][:, z, :],
+                lhsT_scale=w_scales[:, i, z, :],
                 rhs=x_codes[z][:, a:b].bitcast(FP8X4),
                 rhs_scale=x_scales[z][:, a:b],
-                start=(z == 0),
-                stop=(z == PASSES - 1),
+                start=start,
+                stop=stop,
             )
 
-        gather_row(0, 0, S)
-        nc.scalar.activation(row1_bf16[:], rows[1][:], ACT.Copy)
-        nc.scalar.activation(singles[:, 1, LATE:S], row1_bf16[:].indirect(entries(offs_sb, LATE, S)), ACT.Copy)
-        gather_row(1, 0, LATE)
-        place(False, 0, 0, LATE)
-        gather_row(2, 0, S)
+        for j in range(ROWS - 1):
+            gather_row(True, j, 0, ON_VECTOR[j])
+            gather_row(False, j, ON_VECTOR[j], S)
+            if j == 4:
+                for a in range(0, S, BANK):
+                    quantize(0, a, a + BANK)
+            if j % 2 == 1:
+                for a in range(0, S, BANK):
+                    place(j // 2, a, a + BANK)
+
+        banks = {}
+        for i in range(2):
+            for g, parts in enumerate(SUMS):
+                first = min(parts)[0]
+                banks[i, g] = psum.tile([P, max(parts)[1] - first], F32, name=f"bank{i}_{g}")
+                for a, b in parts:
+                    product(banks[i, g][:, a - first : b - first], i, 0, a, b, (a, b) == parts[0], False)
+        h_banks = [psum.tile([P, BANK], F32, name=f"h_bank{g}") for g in range(2)]
+        for g in range(2):
+            product(h_banks[g][:], 2, 0, g * BANK, (g + 1) * BANK, True, False)
+
+        last = ROWS - 1
         for a in range(0, S, PIECE):
-            gather_row(3, a, a + PIECE)
-        for a, b in ((0, PIECE), (PIECE, BANK), (BANK, SCALAR_PLACES)):
-            place(False, 1, a, b)
-        place(True, 1, SCALAR_PLACES, LATE)
-        quantize(0, 0, BANK)
-        quantize(0, BANK, LATE)
-        round_pair(0)
-        woven_late = keep.tile([P, S - LATE, 4], BF16, name="woven_late", tag="both0", align_bytes=64)
-        nc.scalar.activation(woven_late[:], singles[:, :, LATE:S].rearrange("p t n -> p n t"), ACT.Copy)
-        gather(0, 0, S)
-        nc.vector.quantize_mx(
-            out=x_codes[0][:, LATE:S].bitcast(FP8X4),
-            scales=x_scales[0][:, LATE:S],
-            in_=woven_late[:].rearrange("p n t -> p (n t)"),
-        )
-        round_pair(1)
+            gather_row(a == 0, last, a, a + PIECE)
+        place(3, PIECE, BANK)
+        place(3, 0, PIECE)
+        quantize(1, PIECE, BANK)
+        place(3, BANK, S - PIECE)
+        place(3, S - PIECE, S, False)
+        quantize(1, 0, PIECE)
+        for parts in SUMS[1:]:
+            for a, b in parts:
+                quantize(1, a, b)
 
-        banks = [(0, PIECE), (PIECE, BANK)] + [(a, a + NARROW) for a in range(BANK, S, NARROW)]
-        y_ps = [psum.tile([P, b - a], F32, name=f"y_ps{a}", tag=f"bank{g}") for g, (a, b) in enumerate(banks)]
-        for g, (a, b) in enumerate(banks):
-            product(y_ps[g][:, 0:NARROW], 0, 0, a, a + NARROW)
-        e_second = psum.tile([P, BANK], F32, name="e_second")
-        h_second = psum.tile([P, BANK], F32, name="h_second")
-        for a, b in HALVES:
-            nc.tensor.matmul_mx(
-                out=h_second[:],
-                lhsT=w_words[0][:, 0, :].bitcast(FP4X4),
-                lhsT_scale=w_scales[0][:, 0, :],
-                rhs=x_codes[0][:, a:b].bitcast(FP8X4),
-                rhs_scale=x_scales[0][:, a:b],
-                start=True,
-                stop=True,
-            )
-        product(e_second[:], 1, 0, BANK, S)
-        product(h_second[:], 2, 0, BANK, S)
+        for g, parts in enumerate(SUMS):
+            first = min(parts)[0]
+            for a, b in parts:
+                for i in range(2):
+                    product(banks[i, g][:, a - first : b - first], i, 1, a, b, False, (a, b) == parts[-1])
+            if g == 0:
+                product(h_banks[0][:], 2, 1, 0, BANK, False, True)
+        product(h_banks[1][:], 2, 1, BANK, S, False, True)
 
-        for a in range(0, S, PIECE):
-            gather(1, a, a + PIECE)
-        for a, b in ((0, 256), (256, 512), (512, 768), (768, 896), (896, 1024)):
-            weave(a, b)
-        for a, b in ((0, 256), (256, 512), (512, 768), (768, 896), (896, 1024)):
-            quantize(1, a, b)
-        for g, (a, b) in enumerate(banks):
-            product(y_ps[g][:, 0:NARROW], 0, 1, a, a + NARROW)
-            if b - a > NARROW:
-                for z in range(PASSES):
-                    product(y_ps[g][:, NARROW:], 0, z, a + NARROW, b)
-
-        y_sb = keep.tile([P, S], F32, name="y_sb", tag="picked")
-        e_sb = keep.tile([P, S], F32, name="e_sb")
-        h_sb = keep.tile([P, S], F32, name="h_sb")
-        for g, (a, b) in enumerate(banks):
-            if g in (0, 1, 5):
-                nc.scalar.activation(y_sb[:, a:b], y_ps[g][:], ACT.Copy)
-            else:
-                nc.vector.tensor_copy(y_sb[:, a:b], y_ps[g][:])
-        product(e_second[:], 1, 1, BANK, S)
-        nc.scalar.activation(e_sb[:, BANK:S], e_second[:], ACT.Copy)
-        e_first = psum.tile([P, BANK], F32, name="e_first", tag="bank4")
-        for z in range(PASSES):
-            product(e_first[:], 1, z, 0, BANK)
-        nc.scalar.activation(e_sb[:, 0:BANK], e_first[:], ACT.Copy)
-        product(h_second[:], 2, 1, BANK, S)
-        nc.scalar.activation(h_sb[:, BANK:S], h_second[:], ACT.Copy)
-        h_first = psum.tile([P, BANK], F32, name="h_first", tag="bank5")
-        for z in range(PASSES):
-            product(h_first[:], 2, z, 0, BANK)
-        nc.scalar.activation(h_sb[:, 0:BANK], h_first[:], ACT.Copy)
+        y_sb = keep.tile([P, S], F32, name="y_sb")
+        e_sb = keep.tile([P, S], F32, name="e_sb", tag="woven1", align_bytes=64)
+        h_sb = keep.tile([P, S], F32, name="h_sb", tag="x_codes1", align_bytes=64)
+        nc.scalar.activation(y_sb[:, 0:512], banks[0, 0][:], ACT.Copy)
+        nc.scalar.activation(y_sb[:, 512:896], banks[0, 1][:], ACT.Copy)
+        nc.vector.tensor_copy(e_sb[:, 0:512], banks[1, 0][:])
+        nc.vector.tensor_copy(y_sb[:, 896:S], banks[0, 2][:])
+        nc.vector.tensor_copy(e_sb[:, 512:896], banks[1, 1][:])
+        nc.vector.tensor_copy(e_sb[:, 896:S], banks[1, 2][:])
 
         y_dst = keep.tile([P, U], F32, name="y_dst")
         logit = keep.tile([P, U], F32, name="logit")
-        gate = keep.tile([P, U], F32, name="gate", tag="x_codes1", align_bytes=64)
-        for half, (a, b) in enumerate(HALVES):
-            nc.vector.tensor_copy(y_dst[:, a:b], y_sb[:].indirect(entries(dst_sb, a, b)))
-        for a, b in EDGE_PARTS:
+        gate = keep.tile([P, U], F32, name="gate")
+        h_src = keep.tile([P, PIECE], F32, name="h_src")
+        pieces = [(a, a + PIECE) for a in range(0, U, PIECE)]
+        for a, b in pieces:
+            nc.scalar.activation(y_dst[:, a:b], y_sb[:].indirect(entries(dst_sb, a, b)), ACT.Copy)
+        nc.scalar.activation(h_sb[:, BANK:S], h_banks[1][:], ACT.Copy)
+        for a, b in pieces:
             nc.vector.tensor_tensor(logit[:, a:b], e_sb[:].indirect(entries(src_sb, a, b)), y_dst[:, a:b], ALU.add)
+        nc.vector.tensor_copy(h_sb[:, 0:BANK], h_banks[0][:])
+        for a, b in pieces:
             nc.scalar.activation(gate[:, a:b], logit[:, a:b], ACT.Tanh)
-        a = 0
-        for width in EDGE_PIECES:
-            b = a + width
-            message = keep.tile([P, width], F32, name=f"message{a}")
-            nc.vector.tensor_tensor(message[:], h_sb[:].indirect(entries(src_sb, a, b)), gate[:, a:b], ALU.mult)
+        nc.scalar.activation(h_src[:], h_sb[:].indirect(entries(src_sb, U - PIECE, U)), ACT.Copy)
+        for a, b in pieces:
+            message = keep.tile([P, PIECE], F32, name=f"message{a}")
+            if b < U:
+                nc.vector.tensor_tensor(message[:], h_sb[:].indirect(entries(src_sb, a, b)), gate[:, a:b], ALU.mult)
+            else:
+                nc.vector.tensor_tensor(message[:], h_src[:], gate[:, a:b], ALU.mult)
             nc.sync.dma_start(out[:, a:b], message[:])
-            a = b

@@ -22,9 +22,7 @@ ROWS = 4 * PASSES
 LIST_ROWS = 16
 BANK = 512
 PIECE = 256
-NARROW = 128
 ON_VECTOR = (384, 384, 384, 512, 256, 256, 256)
-SUMS = (((256, 512), (0, 256)), ((512, 768), (768, 896)), ((896, 1024),))
 
 
 def tile_picked_edgeatt_tanh_e_kernel(
@@ -67,9 +65,12 @@ def tile_picked_edgeatt_tanh_e_kernel(
 
         for j in range(ROWS):
             if j == ROWS - 1:
+                nc.sync.dma_start(rows[j][:, 0 : T // 2], x_rows[j // 4, j % 4, :, 0 : T // 2])
                 load_words(0)
                 load_words(1)
-            nc.sync.dma_start(rows[j][:], x_rows[j // 4, j % 4])
+                nc.sync.dma_start(rows[j][:, T // 2 : T], x_rows[j // 4, j % 4, :, T // 2 : T])
+            else:
+                nc.sync.dma_start(rows[j][:], x_rows[j // 4, j % 4])
             if j == 0:
                 nc.sync.dma_start(offs_sb[:], offs)
             if 1 <= j <= 6:
@@ -122,67 +123,67 @@ def tile_picked_edgeatt_tanh_e_kernel(
                 for a in range(0, S, BANK):
                     place(j // 2, a, a + BANK)
 
-        banks = {}
-        for i in range(2):
-            for g, parts in enumerate(SUMS):
-                first = min(parts)[0]
-                banks[i, g] = psum.tile([P, max(parts)[1] - first], F32, name=f"bank{i}_{g}")
-                for a, b in parts:
-                    product(banks[i, g][:, a - first : b - first], i, 0, a, b, (a, b) == parts[0], False)
-        h_banks = [psum.tile([P, BANK], F32, name=f"h_bank{g}") for g in range(2)]
-        for g in range(2):
-            product(h_banks[g][:], 2, 0, g * BANK, (g + 1) * BANK, True, False)
+        pieces = [(a, a + PIECE) for a in range(0, S, PIECE)]
+        halves = [(a, a + BANK) for a in range(0, S, BANK)]
+        y_banks = [psum.tile([P, PIECE], F32, name=f"y_bank{a}") for a, b in pieces]
+        e_banks = [psum.tile([P, BANK], F32, name=f"e_bank{a}") for a, b in halves]
+        h_banks = [psum.tile([P, BANK], F32, name=f"h_bank{a}") for a, b in halves]
+        for g, (a, b) in enumerate(pieces):
+            product(y_banks[g][:], 0, 0, a, b, True, False)
+        for i, banks in ((1, e_banks), (2, h_banks)):
+            for g, (a, b) in enumerate(halves):
+                product(banks[g][:], i, 0, a, b, True, False)
 
         last = ROWS - 1
-        for a in range(0, S, PIECE):
-            gather_row(a == 0, last, a, a + PIECE)
-        place(3, PIECE, BANK)
-        place(3, 0, PIECE)
-        quantize(1, PIECE, BANK)
-        place(3, BANK, S - PIECE)
-        place(3, S - PIECE, S, False)
-        quantize(1, 0, PIECE)
-        for parts in SUMS[1:]:
-            for a, b in parts:
-                quantize(1, a, b)
+        for g in (0, 1, 3, 2):
+            gather_row(g == 1, last, *pieces[g])
+        place(3, *pieces[0])
+        place(3, *pieces[1])
+        place(3, *pieces[3], False)
+        quantize(1, *pieces[0])
+        quantize(1, *pieces[1])
+        place(3, *pieces[2])
+        order = (0, 1, 3, 2)
+        for g in order[2:]:
+            quantize(1, *pieces[g])
 
-        for g, parts in enumerate(SUMS):
-            first = min(parts)[0]
-            for a, b in parts:
-                for i in range(2):
-                    product(banks[i, g][:, a - first : b - first], i, 1, a, b, False, (a, b) == parts[-1])
-            if g == 0:
-                product(h_banks[0][:], 2, 1, 0, BANK, False, True)
-        product(h_banks[1][:], 2, 1, BANK, S, False, True)
+        for n, g in enumerate(order):
+            a, b = pieces[g]
+            product(y_banks[g][:], 0, 1, a, b, False, True)
+            product(e_banks[g // 2][:, a % BANK : a % BANK + PIECE], 1, 1, a, b, False, n % 2 == 1)
+            if n % 2 == 1:
+                product(h_banks[g // 2][:], 2, 1, *halves[g // 2], False, True)
 
         y_sb = keep.tile([P, S], F32, name="y_sb")
-        e_sb = keep.tile([P, S], F32, name="e_sb", tag="woven1", align_bytes=64)
-        h_sb = keep.tile([P, S], F32, name="h_sb", tag="x_codes1", align_bytes=64)
-        nc.scalar.activation(y_sb[:, 0:512], banks[0, 0][:], ACT.Copy)
-        nc.scalar.activation(y_sb[:, 512:896], banks[0, 1][:], ACT.Copy)
-        nc.vector.tensor_copy(e_sb[:, 0:512], banks[1, 0][:])
-        nc.vector.tensor_copy(y_sb[:, 896:S], banks[0, 2][:])
-        nc.vector.tensor_copy(e_sb[:, 512:896], banks[1, 1][:])
-        nc.vector.tensor_copy(e_sb[:, 896:S], banks[1, 2][:])
+        e_sb = keep.tile([P, S], F32, name="e_sb")
+        h_sb = keep.tile([P, S], F32, name="h_sb")
+        for n, g in enumerate(order):
+            a, b = pieces[g]
+            nc.scalar.activation(y_sb[:, a:b], y_banks[g][:], ACT.Copy)
+            if n == 1:
+                nc.scalar.activation(e_sb[:, 0:BANK], e_banks[0][:], ACT.Copy)
+        nc.vector.tensor_copy(h_sb[:, 0:BANK], h_banks[0][:])
+        nc.vector.tensor_copy(e_sb[:, BANK:S], e_banks[1][:])
+        nc.scalar.activation(h_sb[:, BANK:S], h_banks[1][:], ACT.Copy)
 
         y_dst = keep.tile([P, U], F32, name="y_dst")
         logit = keep.tile([P, U], F32, name="logit")
         gate = keep.tile([P, U], F32, name="gate")
-        h_src = keep.tile([P, PIECE], F32, name="h_src")
-        pieces = [(a, a + PIECE) for a in range(0, U, PIECE)]
-        for a, b in pieces:
+        h_src = keep.tile([P, BANK], F32, name="h_src")
+        nc.vector.tensor_copy(y_dst[:, 0:PIECE], y_sb[:].indirect(entries(dst_sb, 0, PIECE)))
+        for a, b in pieces[1:]:
             nc.scalar.activation(y_dst[:, a:b], y_sb[:].indirect(entries(dst_sb, a, b)), ACT.Copy)
-        nc.scalar.activation(h_sb[:, BANK:S], h_banks[1][:], ACT.Copy)
         for a, b in pieces:
             nc.vector.tensor_tensor(logit[:, a:b], e_sb[:].indirect(entries(src_sb, a, b)), y_dst[:, a:b], ALU.add)
-        nc.vector.tensor_copy(h_sb[:, 0:BANK], h_banks[0][:])
-        for a, b in pieces:
+        for a, b in pieces[:2]:
             nc.scalar.activation(gate[:, a:b], logit[:, a:b], ACT.Tanh)
-        nc.scalar.activation(h_src[:], h_sb[:].indirect(entries(src_sb, U - PIECE, U)), ACT.Copy)
+        for a, b in pieces[2:]:
+            nc.scalar.activation(gate[:, a:b], logit[:, a:b], ACT.Tanh)
+            nc.scalar.activation(h_src[:, a - BANK : b - BANK], h_sb[:].indirect(entries(src_sb, a, b)), ACT.Copy)
         for a, b in pieces:
             message = keep.tile([P, PIECE], F32, name=f"message{a}")
-            if b < U:
+            if a < BANK:
                 nc.vector.tensor_tensor(message[:], h_sb[:].indirect(entries(src_sb, a, b)), gate[:, a:b], ALU.mult)
             else:
-                nc.vector.tensor_tensor(message[:], h_src[:], gate[:, a:b], ALU.mult)
+                nc.vector.tensor_tensor(message[:], h_src[:, a - BANK : b - BANK], gate[:, a:b], ALU.mult)
             nc.sync.dma_start(out[:, a:b], message[:])

@@ -22,7 +22,8 @@ ROWS = 4 * PASSES
 LIST_ROWS = 16
 BANK = 512
 PIECE = 256
-ON_VECTOR = (384, 384, 384, 512, 256, 256, 256)
+ON_VECTOR = (512, 256, 512, 256, 256, 256)
+IN_PLACE = 384
 
 
 def tile_picked_edgeatt_tanh_e_kernel(
@@ -113,17 +114,27 @@ def tile_picked_edgeatt_tanh_e_kernel(
                 stop=stop,
             )
 
-        for j in range(ROWS - 1):
+        def gather_in_place(j, a, b):
+            into = woven[j // 4][:].rearrange("p (n t) -> p n t", t=4)[:, a:b, j % 4]
+            nc.vector.tensor_copy(into, rows[j][:].indirect(entries(offs_sb, a, b)))
+
+        for j in range(ROWS - 2):
             gather_row(True, j, 0, ON_VECTOR[j])
-            gather_row(False, j, ON_VECTOR[j], S)
+            if j % 2 == 0:
+                gather_row(False, j, ON_VECTOR[j], S)
+            else:
+                for a in range(PIECE, S, PIECE):
+                    gather_row(False, j, a, a + PIECE)
+                place(j // 2, 0, BANK)
+                for a in range(BANK, S, PIECE):
+                    place(j // 2, a, a + PIECE)
             if j == 4:
                 for a in range(0, S, BANK):
                     quantize(0, a, a + BANK)
-            if j % 2 == 1:
-                for a in range(0, S, BANK):
-                    place(j // 2, a, a + BANK)
 
         pieces = [(a, a + PIECE) for a in range(0, S, PIECE)]
+        gather_in_place(ROWS - 2, 0, IN_PLACE)
+        gather_row(False, ROWS - 2, IN_PLACE, S)
         halves = [(a, a + BANK) for a in range(0, S, BANK)]
         y_banks = [psum.tile([P, PIECE], F32, name=f"y_bank{a}") for a, b in pieces]
         e_banks = [psum.tile([P, BANK], F32, name=f"e_bank{a}") for a, b in halves]
@@ -135,10 +146,11 @@ def tile_picked_edgeatt_tanh_e_kernel(
                 product(banks[g][:], i, 0, a, b, True, False)
 
         last = ROWS - 1
-        for g in (0, 1, 3, 2):
-            gather_row(g == 1, last, *pieces[g])
-        place(3, *pieces[0])
-        place(3, *pieces[1])
+        gather_in_place(last, 0, IN_PLACE)
+        gather_row(False, last, IN_PLACE, BANK)
+        gather_row(False, last, *pieces[3])
+        gather_row(False, last, *pieces[2])
+        place(3, IN_PLACE, BANK)
         place(3, *pieces[3], False)
         quantize(1, *pieces[0])
         quantize(1, *pieces[1])
@@ -175,11 +187,15 @@ def tile_picked_edgeatt_tanh_e_kernel(
             nc.scalar.activation(y_dst[:, a:b], y_sb[:].indirect(entries(dst_sb, a, b)), ACT.Copy)
         for a, b in pieces:
             nc.vector.tensor_tensor(logit[:, a:b], e_sb[:].indirect(entries(src_sb, a, b)), y_dst[:, a:b], ALU.add)
-        for a, b in pieces[:2]:
-            nc.scalar.activation(gate[:, a:b], logit[:, a:b], ACT.Tanh)
-        for a, b in pieces[2:]:
-            nc.scalar.activation(gate[:, a:b], logit[:, a:b], ACT.Tanh)
+
+        def gather_h(a, b):
             nc.scalar.activation(h_src[:, a - BANK : b - BANK], h_sb[:].indirect(entries(src_sb, a, b)), ACT.Copy)
+
+        gather_h(*pieces[2])
+        for a, b in pieces[:3]:
+            nc.scalar.activation(gate[:, a:b], logit[:, a:b], ACT.Tanh)
+        gather_h(*pieces[3])
+        nc.scalar.activation(gate[:, pieces[3][0] : S], logit[:, pieces[3][0] : S], ACT.Tanh)
         for a, b in pieces:
             message = keep.tile([P, PIECE], F32, name=f"message{a}")
             if a < BANK:

@@ -69,16 +69,16 @@ def tile_picked_edgeatt_tanh_e_kernel(
                 nc.sync.dma_start(rows[j][:, 0 : T // 2], x_rows[j // 4, j % 4, :, 0 : T // 2])
                 load_words(0)
                 load_words(1)
+                load_words(2)
                 nc.sync.dma_start(rows[j][:, T // 2 : T], x_rows[j // 4, j % 4, :, T // 2 : T])
             else:
                 nc.sync.dma_start(rows[j][:], x_rows[j // 4, j % 4])
             if j == 0:
                 nc.sync.dma_start(offs_sb[:], offs)
+                nc.sync.dma_start(dst_sb[:], dst)
+                nc.sync.dma_start(src_sb[:], src)
             if 1 <= j <= 6:
                 load_scale_rows((j - 1) // 2, range(2 * ((j - 1) % 2), 2 * ((j - 1) % 2) + 2))
-        load_words(2)
-        nc.sync.dma_start(dst_sb[:], dst)
-        nc.sync.dma_start(src_sb[:], src)
 
         def gather_row(on_vector, j, a, b):
             into = picked[j // 2][:, j % 2, a:b]

@@ -24,6 +24,7 @@ BANK = 512
 PIECE = 256
 ON_VECTOR = (512, 256, 512, 256, 256, 256)
 IN_PLACE = 384
+EDGE_CUTS = (0, 256, 576, 832, 1024)
 
 
 def tile_picked_edgeatt_tanh_e_kernel(
@@ -75,10 +76,10 @@ def tile_picked_edgeatt_tanh_e_kernel(
                 nc.sync.dma_start(rows[j][:], x_rows[j // 4, j % 4])
             if j == 0:
                 nc.sync.dma_start(offs_sb[:], offs)
-                nc.sync.dma_start(dst_sb[:], dst)
-                nc.sync.dma_start(src_sb[:], src)
             if 1 <= j <= 6:
                 load_scale_rows((j - 1) // 2, range(2 * ((j - 1) % 2), 2 * ((j - 1) % 2) + 2))
+        nc.sync.dma_start(dst_sb[:], dst)
+        nc.sync.dma_start(src_sb[:], src)
 
         def gather_row(on_vector, j, a, b):
             into = picked[j // 2][:, j % 2, a:b]
@@ -181,25 +182,32 @@ def tile_picked_edgeatt_tanh_e_kernel(
         y_dst = keep.tile([P, U], F32, name="y_dst")
         logit = keep.tile([P, U], F32, name="logit")
         gate = keep.tile([P, U], F32, name="gate")
-        h_src = keep.tile([P, BANK], F32, name="h_src")
-        nc.vector.tensor_copy(y_dst[:, 0:PIECE], y_sb[:].indirect(entries(dst_sb, 0, PIECE)))
-        for a, b in pieces[1:]:
+        h_src = keep.tile([P, U], F32, name="h_src")
+        parts = list(zip(EDGE_CUTS, EDGE_CUTS[1:]))
+        first_halves = [(0, EDGE_CUTS[1] // 2), (EDGE_CUTS[1] // 2, EDGE_CUTS[1])]
+        for a, b in first_halves:
+            nc.vector.tensor_copy(y_dst[:, a:b], y_sb[:].indirect(entries(dst_sb, a, b)))
+        for a, b in parts[1:]:
             nc.scalar.activation(y_dst[:, a:b], y_sb[:].indirect(entries(dst_sb, a, b)), ACT.Copy)
-        for a, b in pieces:
+        for a, b in first_halves + parts[1:]:
             nc.vector.tensor_tensor(logit[:, a:b], e_sb[:].indirect(entries(src_sb, a, b)), y_dst[:, a:b], ALU.add)
 
-        def gather_h(a, b):
-            nc.scalar.activation(h_src[:, a - BANK : b - BANK], h_sb[:].indirect(entries(src_sb, a, b)), ACT.Copy)
-
-        gather_h(*pieces[2])
-        for a, b in pieces[:3]:
+        def tanh(a, b):
             nc.scalar.activation(gate[:, a:b], logit[:, a:b], ACT.Tanh)
-        gather_h(*pieces[3])
-        nc.scalar.activation(gate[:, pieces[3][0] : S], logit[:, pieces[3][0] : S], ACT.Tanh)
-        for a, b in pieces:
-            message = keep.tile([P, PIECE], F32, name=f"message{a}")
-            if a < BANK:
+
+        def gather_h(a, b):
+            nc.scalar.activation(h_src[:, a:b], h_sb[:].indirect(entries(src_sb, a, b)), ACT.Copy)
+
+        tanh(*parts[0])
+        gather_h(*parts[2])
+        tanh(*parts[1])
+        tanh(*parts[2])
+        gather_h(*parts[3])
+        tanh(*parts[3])
+        for n, (a, b) in enumerate(parts):
+            message = keep.tile([P, b - a], F32, name=f"message{a}")
+            if n < 2:
                 nc.vector.tensor_tensor(message[:], h_sb[:].indirect(entries(src_sb, a, b)), gate[:, a:b], ALU.mult)
             else:
-                nc.vector.tensor_tensor(message[:], h_src[:, a - BANK : b - BANK], gate[:, a:b], ALU.mult)
+                nc.vector.tensor_tensor(message[:], h_src[:, a:b], gate[:, a:b], ALU.mult)
             nc.sync.dma_start(out[:, a:b], message[:])

@@ -54,8 +54,9 @@ def tile_picked_edgeatt_tanh_e_kernel(
                     weights[i][1][:, 4 * q : 4 * q + 4, :].rearrange("z r c -> r z c").bitcast(I32),
                 )
 
-        def load_words(i):
-            nc.sync.dma_start(w_words[i][:].bitcast(I32), weights[i][0].rearrange("z p b -> p z b").bitcast(I32))
+        def load_words(i, first=0, end=PASSES):
+            words = weights[i][0].rearrange("z p b -> p z b")
+            nc.sync.dma_start(w_words[i][:, first:end].bitcast(I32), words[:, first:end].bitcast(I32))
 
 
         x_rows = xT.rearrange("(z p t) n -> z t p n", z=PASSES, p=P, t=4)
@@ -68,10 +69,11 @@ def tile_picked_edgeatt_tanh_e_kernel(
         for j in range(ROWS):
             if j == ROWS - 1:
                 nc.sync.dma_start(rows[j][:, 0 : T // 2], x_rows[j // 4, j % 4, :, 0 : T // 2])
-                load_words(0)
+                load_words(0, 0, 1)
                 load_words(1)
-                load_words(2)
                 nc.sync.dma_start(rows[j][:, T // 2 : T], x_rows[j // 4, j % 4, :, T // 2 : T])
+                load_words(2)
+                load_words(0, 1, 2)
             else:
                 nc.sync.dma_start(rows[j][:], x_rows[j // 4, j % 4])
             if j == 0:

from contextlib import ExitStack

import concourse.mybir as mybir

K, T, S, N, U = 1024, 2048, 1024, 128, 1024
FLOPS = 3 * 2 * K * N * S

F32 = mybir.dt.float32
BF16 = mybir.dt.bfloat16
U32 = mybir.dt.uint32
I32 = mybir.dt.int32
U16 = mybir.dt.uint16
U8 = mybir.dt.uint8
FP8X4 = mybir.dt.float8_e4m3fn_x4
FP4X4 = mybir.dt.float4_e2m1fn_x4
ACT = mybir.ActivationFunctionType
ALU = mybir.AluOpType

P = 128
PASSES = K // 512
ROWS = 4 * PASSES
LIST_ROWS = 16
BANK = 512
PIECE = 256
ON_VECTOR = (512, 256, 512, 256, 256, 256)
IN_PLACE = 384
EDGE_CUTS = (0, 256, 576, 832, 1024)


def tile_picked_edgeatt_tanh_e_kernel(
    tc, xT, w1_words, w1_scales, w2_words, w2_scales, w3_words, w3_scales, offs, src, dst, out
):
    nc = tc.nc
    with ExitStack() as ctx:
        keep = ctx.enter_context(tc.tile_pool(name="keep", bufs=1))
        psum = ctx.enter_context(tc.psum_pool(name="psum", bufs=1))

        offs_sb = keep.tile([P, S // LIST_ROWS], U16, name="offs_sb")
        src_sb = keep.tile([P, U // LIST_ROWS], U16, name="src_sb")
        dst_sb = keep.tile([P, U // LIST_ROWS], U16, name="dst_sb")

        def entries(list_sb, a, b):
            return list_sb[:, a // LIST_ROWS : b // LIST_ROWS]

        w_words = [keep.tile([P, PASSES, 2 * N], U8, name=f"w_words{i}", align_bytes=64) for i in range(3)]
        w_scales = keep.tile([P, 3, PASSES, N], U8, name="w_scales", align_bytes=64)
        nc.gpsimd.memset(w_scales[:].rearrange("p i z c -> p (i z c)").bitcast(I32), 0)
        weights = ((w1_words, w1_scales), (w2_words, w2_scales), (w3_words, w3_scales))

        def load_scale_rows(i, quadrants):
            for q in quadrants:
                nc.sync.dma_start(
                    w_scales[32 * q : 32 * q + 4, i].bitcast(I32),
                    weights[i][1][:, 4 * q : 4 * q + 4, :].rearrange("z r c -> r z c").bitcast(I32),
                )

        def load_words(i, first=0, end=PASSES):
            words = weights[i][0].rearrange("z p b -> p z b")
            nc.sync.dma_start(w_words[i][:, first:end].bitcast(I32), words[:, first:end].bitcast(I32))


        x_rows = xT.rearrange("(z p t) n -> z t p n", z=PASSES, p=P, t=4)
        rows = [keep.tile([P, T], F32, name=f"rows{j}") for j in range(ROWS)]
        picked = [keep.tile([P, 2, S], BF16, name=f"picked{u}") for u in range(ROWS // 2)]
        woven = [keep.tile([P, 4 * S], BF16, name=f"woven{z}", tag=f"woven{z}", align_bytes=64) for z in range(PASSES)]
        x_codes = [keep.tile([P, S], U32, name=f"x_codes{z}", tag=f"x_codes{z}", align_bytes=64) for z in range(PASSES)]
        x_scales = [keep.tile([P, S], U8, name=f"x_scales{z}", align_bytes=64) for z in range(PASSES)]

        for j in range(ROWS):
            if j == ROWS - 1:
                nc.sync.dma_start(rows[j][:, 0 : T // 2], x_rows[j // 4, j % 4, :, 0 : T // 2])
                load_words(0, 0, 1)
                load_words(1)
                nc.sync.dma_start(rows[j][:, T // 2 : T], x_rows[j // 4, j % 4, :, T // 2 : T])
                load_words(2)
                load_words(0, 1, 2)
            else:
                nc.sync.dma_start(rows[j][:], x_rows[j // 4, j % 4])
            if j == 0:
                nc.sync.dma_start(offs_sb[:], offs)
            if 1 <= j <= 6:
                load_scale_rows((j - 1) // 2, range(2 * ((j - 1) % 2), 2 * ((j - 1) % 2) + 2))
        nc.sync.dma_start(dst_sb[:], dst)
        nc.sync.dma_start(src_sb[:], src)

        def gather_row(on_vector, j, a, b):
            into = picked[j // 2][:, j % 2, a:b]
            values = rows[j][:].indirect(entries(offs_sb, a, b))
            if on_vector:
                nc.vector.tensor_copy(into, values)
            else:
                nc.scalar.activation(into, values, ACT.Copy)

        def place(u, a, b, on_vector=True):
            into = woven[u // 2][:].rearrange("p (n t) -> p n t", t=4)[:, a:b, 2 * (u % 2) : 2 * (u % 2) + 2]
            values = picked[u][:, :, a:b].rearrange("p e n -> p n e")
            if on_vector:
                nc.vector.tensor_copy(into, values)
            else:
                nc.scalar.activation(into, values, ACT.Copy)

        def quantize(z, a, b):
            nc.vector.quantize_mx(
                out=x_codes[z][:, a:b].bitcast(FP8X4),
                scales=x_scales[z][:, a:b],
                in_=woven[z][:, 4 * a : 4 * b],
            )

        def product(acc, i, z, a, b, start, stop):
            nc.tensor.matmul_mx(
                out=acc,
                lhsT=w_words[i][:, z, :].bitcast(FP4X4),
                lhsT_scale=w_scales[:, i, z, :],
                rhs=x_codes[z][:, a:b].bitcast(FP8X4),
                rhs_scale=x_scales[z][:, a:b],
                start=start,
                stop=stop,
            )

        def gather_in_place(j, a, b):
            into = woven[j // 4][:].rearrange("p (n t) -> p n t", t=4)[:, a:b, j % 4]
            nc.vector.tensor_copy(into, rows[j][:].indirect(entries(offs_sb, a, b)))

        for j in range(ROWS - 2):
            gather_row(True, j, 0, ON_VECTOR[j])
            if j % 2 == 0:
                gather_row(False, j, ON_VECTOR[j], S)
            else:
                for a in range(PIECE, S, PIECE):
                    gather_row(False, j, a, a + PIECE)
                place(j // 2, 0, BANK)
                for a in range(BANK, S, PIECE):
                    place(j // 2, a, a + PIECE)
            if j == 4:
                for a in range(0, S, BANK):
                    quantize(0, a, a + BANK)

        pieces = [(a, a + PIECE) for a in range(0, S, PIECE)]
        gather_in_place(ROWS - 2, 0, IN_PLACE)
        gather_row(False, ROWS - 2, IN_PLACE, S)
        halves = [(a, a + BANK) for a in range(0, S, BANK)]
        y_banks = [psum.tile([P, PIECE], F32, name=f"y_bank{a}") for a, b in pieces]
        e_banks = [psum.tile([P, BANK], F32, name=f"e_bank{a}") for a, b in halves]
        h_banks = [psum.tile([P, BANK], F32, name=f"h_bank{a}") for a, b in halves]
        for g, (a, b) in enumerate(pieces):
            product(y_banks[g][:], 0, 0, a, b, True, False)
        for i, banks in ((1, e_banks), (2, h_banks)):
            for g, (a, b) in enumerate(halves):
                product(banks[g][:], i, 0, a, b, True, False)

        last = ROWS - 1
        gather_in_place(last, 0, IN_PLACE)
        gather_row(False, last, IN_PLACE, BANK)
        gather_row(False, last, *pieces[3])
        gather_row(False, last, *pieces[2])
        place(3, IN_PLACE, BANK)
        place(3, *pieces[3], False)
        quantize(1, *pieces[0])
        quantize(1, *pieces[1])
        place(3, *pieces[2])
        order = (0, 1, 3, 2)
        for g in order[2:]:
            quantize(1, *pieces[g])

        for n, g in enumerate(order):
            a, b = pieces[g]
            product(y_banks[g][:], 0, 1, a, b, False, True)
            product(e_banks[g // 2][:, a % BANK : a % BANK + PIECE], 1, 1, a, b, False, n % 2 == 1)
            if n % 2 == 1:
                product(h_banks[g // 2][:], 2, 1, *halves[g // 2], False, True)

        y_sb = keep.tile([P, S], F32, name="y_sb")
        e_sb = keep.tile([P, S], F32, name="e_sb")
        h_sb = keep.tile([P, S], F32, name="h_sb")
        for n, g in enumerate(order):
            a, b = pieces[g]
            nc.scalar.activation(y_sb[:, a:b], y_banks[g][:], ACT.Copy)
            if n == 1:
                nc.scalar.activation(e_sb[:, 0:BANK], e_banks[0][:], ACT.Copy)
        nc.vector.tensor_copy(h_sb[:, 0:BANK], h_banks[0][:])
        nc.vector.tensor_copy(e_sb[:, BANK:S], e_banks[1][:])
        nc.scalar.activation(h_sb[:, BANK:S], h_banks[1][:], ACT.Copy)

        y_dst = keep.tile([P, U], F32, name="y_dst")
        logit = keep.tile([P, U], F32, name="logit")
        gate = keep.tile([P, U], F32, name="gate")
        h_src = keep.tile([P, U], F32, name="h_src")
        parts = list(zip(EDGE_CUTS, EDGE_CUTS[1:]))
        first_halves = [(0, EDGE_CUTS[1] // 2), (EDGE_CUTS[1] // 2, EDGE_CUTS[1])]
        for a, b in first_halves:
            nc.vector.tensor_copy(y_dst[:, a:b], y_sb[:].indirect(entries(dst_sb, a, b)))
        for a, b in parts[1:]:
            nc.scalar.activation(y_dst[:, a:b], y_sb[:].indirect(entries(dst_sb, a, b)), ACT.Copy)
        for a, b in first_halves + parts[1:]:
            nc.vector.tensor_tensor(logit[:, a:b], e_sb[:].indirect(entries(src_sb, a, b)), y_dst[:, a:b], ALU.add)

        def tanh(a, b):
            nc.scalar.activation(gate[:, a:b], logit[:, a:b], ACT.Tanh)

        def gather_h(a, b):
            nc.scalar.activation(h_src[:, a:b], h_sb[:].indirect(entries(src_sb, a, b)), ACT.Copy)

        tanh(*parts[0])
        gather_h(*parts[2])
        tanh(*parts[1])
        tanh(*parts[2])
        gather_h(*parts[3])
        tanh(*parts[3])
        for n, (a, b) in enumerate(parts):
            message = keep.tile([P, b - a], F32, name=f"message{a}")
            if n < 2:
                nc.vector.tensor_tensor(message[:], h_sb[:].indirect(entries(src_sb, a, b)), gate[:, a:b], ALU.mult)
            else:
                nc.vector.tensor_tensor(message[:], h_src[:, a:b], gate[:, a:b], ALU.mult)
            nc.sync.dma_start(out[:, a:b], message[:])
